import numpy as np
import ml_dtypes


def mxq(x, axis, fmt="e4m3"):
    dtype, down = {"e4m3": (ml_dtypes.float8_e4m3fn, 7), "e5m2": (ml_dtypes.float8_e5m2, 14)}[fmt]
    v = np.moveaxis(np.asarray(x, np.float32).astype(ml_dtypes.bfloat16).astype(np.float64), axis, -1)
    blocks = v.reshape(v.shape[:-1] + (-1, 32))
    amax = np.abs(blocks).max(-1, keepdims=True)
    byte = np.maximum(np.where(amax > 0, np.frexp(amax)[1] - 1 + 127, 0) - down, 1)
    scale = np.exp2(byte - 127.0)
    codes = (blocks / scale).astype(np.float32).astype(dtype).astype(np.float64)
    return np.moveaxis((codes * scale).reshape(v.shape), -1, axis)


WIDE = False


def mx_kscale(k):
    if not WIDE:
        return np.ones(k)
    levels = np.array([24, -24, 12, -12, 0])
    if k % 512:
        return np.exp2(np.random.permutation(np.resize(levels, k // 32))).repeat(32)
    a = np.empty((k // 512, 16))
    for p in range(k // 512):
        a[p, :8] = np.random.permutation(np.resize(levels, 8))
        for g in range(8):
            far = levels[np.abs(levels - a[p, g]) >= 10]
            a[p, g + 8] = far[np.random.randint(len(far))]
    return np.exp2(a.ravel()).repeat(32)


def f64(x):
    return np.asarray(x).astype(np.float64)


def striped(idx):
    return np.tile(idx.reshape(-1, 16).T, (8, 1)).astype(np.uint16)


def unstriped(offs):
    return offs[:16].T.reshape(-1).astype(np.int64)


E2M1 = np.array([0.0, 0.5, 1.0, 1.5, 2.0, 3.0, 4.0, 6.0, -0.0, -0.5, -1.0, -1.5, -2.0, -3.0, -4.0, -6.0])


def pack_weight(w, fmt):
    k, n = w.shape
    w = f64(np.asarray(w, np.float32).astype(ml_dtypes.bfloat16)).reshape(k // 32, 32, n)
    amax = np.abs(w).max(1)
    if fmt == "e4m3":
        byte = np.frexp(amax)[1] - 1 + 127 - 7
    else:
        mant, ex = np.frexp(amax / 6.0)
        byte = np.where(mant > 0.5, ex, ex - 1) + 127
    byte = np.clip(np.where(amax > 0, byte, 1), 1, 254)
    scaled = (w * np.exp2(127.0 - byte)[:, None, :]).reshape(k, n).astype(np.float32)
    by_word = np.ascontiguousarray(scaled.reshape(k // 512, 128, 4, n).transpose(0, 1, 3, 2))
    if fmt == "e4m3":
        words = by_word.astype(ml_dtypes.float8_e4m3fn).view(np.uint8)
    else:
        c = by_word.astype(ml_dtypes.float4_e2m1fn).view(np.uint8) & 0xF
        words = (c[..., 0::2] | (c[..., 1::2] << 4)).reshape(k // 512, 128, 2 * n)
    return np.ascontiguousarray(words), np.ascontiguousarray(byte.astype(np.uint8).reshape(k // 512, 16, n))


def unpack_weight(words, scales, fmt):
    g, _, n = scales.shape
    words = np.ascontiguousarray(words).reshape(g, 128, n, -1)
    if fmt == "e4m3":
        vals = words.view(ml_dtypes.float8_e4m3fn).astype(np.float64)
    else:
        nib = np.empty((g, 128, n, 4), np.uint8)
        nib[..., 0::2] = words & 0xF
        nib[..., 1::2] = words >> 4
        vals = E2M1[nib]
    vals = vals * np.repeat(np.exp2(scales.astype(np.float64) - 127.0), 8, axis=1)[..., None]
    return vals.transpose(0, 1, 3, 2).reshape(g * 512, n)


def pack_table4(v):
    words, scales = pack_weight(v, "e2m1")
    g, t = words.shape[0] // 2, v.shape[1]
    return np.ascontiguousarray(words.reshape(g, 2, 128, t, 2).transpose(0, 2, 3, 1, 4).reshape(g, 128, t, 4)), scales


def unpack_table4(words, scales):
    g, _, t, _ = words.shape
    return unpack_weight(words.reshape(g, 128, t, 2, 2).transpose(0, 3, 1, 2, 4).reshape(2 * g, 128, 2 * t), scales, "e2m1")


def planes(y):
    n, m = y.shape
    v = y.astype(np.float32).astype(ml_dtypes.bfloat16).astype(np.float64).reshape(n // 32, 32, m)
    top = np.abs(v).max(1)
    byte = np.clip(np.where(top > 0, np.frexp(top)[1] - 1 + 127 - 7, 1), 1, 254)
    codes = (v * np.exp2(127.0 - byte)[:, None, :]).reshape(n, m).astype(np.float32).astype(ml_dtypes.float8_e4m3fn).view(np.uint8)
    words = codes.reshape(n // 512, 128, 4, m).transpose(0, 1, 3, 2)
    return np.ascontiguousarray(words), np.ascontiguousarray(byte.astype(np.uint8).reshape(n // 512, 16, m))


def sigm(f):
    return 1.0 / (1.0 + np.exp(-np.maximum(f, -700.0)))


K, R, N, T, J = 1024, 512, 512, 4096, 1024


def setup_inputs():
    n = np.random.standard_normal
    s = mx_kscale(K)[:, None]
    u = mx_kscale(R)[:, None]
    p_tab = pack_table4(n((K, T)) * s)
    p_wg = pack_weight(n((K, R)) / np.sqrt(K) / s, "e2m1")
    p_wu = pack_weight(n((K, R)) / np.sqrt(K) / s * u.T, "e4m3")
    p_wd = pack_weight(n((R, N)) / np.sqrt(R) / u, "e4m3")
    return {
        "tab_words": p_tab[0],
        "tab_scales": p_tab[1],
        "wg_words": p_wg[0],
        "wg_scales": p_wg[1],
        "wu_words": p_wu[0],
        "wu_scales": p_wu[1],
        "wd_words": p_wd[0],
        "wd_scales": p_wd[1],
        "rT": (n((N, T))).astype(np.float32),
        "offs": striped(np.random.permutation(T)[:J]),
    }


def reference(tab_words, tab_scales, wg_words, wg_scales, wu_words, wu_scales, wd_words, wd_scales, rT, offs):
    idx = unstriped(offs)
    tab_ = unpack_table4(tab_words, tab_scales)[:, idx]
    wg_ = unpack_weight(wg_words, wg_scales, "e2m1")
    wu_ = unpack_weight(wu_words, wu_scales, "e4m3")
    ga = wg_.T @ tab_
    ub = wu_.T @ tab_
    h = sigm(ga) * ub
    h_ = mxq(h, 0, "e4m3")
    wd_ = unpack_weight(wd_words, wd_scales, "e4m3")
    y = wd_.T @ h_
    out_0 = y + f64(rT)[:, idx]
    return (out_0,) + planes(out_0)

@@ -1,0 +1,208 @@
+from contextlib import ExitStack
+
+import concourse.mybir as mybir
+from concourse.masks import make_identity
+
+K, R, N, T, J = 1024, 512, 512, 4096, 1024
+FLOPS = 2 * J * (2 * K * R + R * N)
+
+F32 = mybir.dt.float32
+BF16 = mybir.dt.bfloat16
+I32 = mybir.dt.int32
+U32 = mybir.dt.uint32
+U16 = mybir.dt.uint16
+U8 = mybir.dt.uint8
+FP8X4 = mybir.dt.float8_e4m3fn_x4
+FP4X4 = mybir.dt.float4_e2m1fn_x4
+ADD = mybir.AluOpType.add
+MULT = mybir.AluOpType.mult
+SIGMOID = mybir.ActivationFunctionType.Sigmoid
+
+P = 128
+HALF = 512
+TAIL = 256
+
+
+def tile_list_gmlpt_sigm_resLP_kernel(
+    tc, tab_words, tab_scales, wg_words, wg_scales, wu_words, wu_scales, wd_words, wd_scales, rT, offs,
+    out_0, out_1, out_2,
+):
+    nc = tc.nc
+    with ExitStack() as ctx:
+        keep = ctx.enter_context(tc.tile_pool(name="keep", bufs=1))
+        ring = ctx.enter_context(tc.tile_pool(name="ring", bufs=4))
+        psum = ctx.enter_context(tc.psum_pool(name="psum", bufs=2))
+
+        offsets = keep.tile([P, J // 16], U16, name="offsets")
+        nc.sync.dma_start(offsets[:], offs)
+
+        def cols(first, count):
+            return offsets[:, first // 16 : (first + count) // 16]
+
+
+        tsc = keep.tile([P, T], U8, name="tsc", align_bytes=64)
+        gsc = keep.tile([P, 2, R], U8, name="gsc", align_bytes=64)
+        usc = keep.tile([P, 2, R], U8, name="usc", align_bytes=64)
+        dsc = keep.tile([P, N], U8, name="dsc", align_bytes=64)
+        vsc = keep.tile([P, 2, J], U8, name="vsc", align_bytes=64)
+        nc.gpsimd.memset(usc[:].bitcast(I32), 0)
+        nc.vector.memset(tsc[:].bitcast(I32), 0)
+        nc.vector.memset(gsc[:].bitcast(I32), 0)
+        nc.vector.memset(dsc[:].bitcast(I32), 0)
+        nc.vector.memset(vsc[:].bitcast(I32), 0)
+
+        def load_scales(queue, tile, dram):
+            for q in range(4):
+                queue.dma_start(tile[32 * q : 32 * q + 4].bitcast(I32),
+                                dram[:, 4 * q : 4 * q + 4, :].rearrange("a r n -> r a n").bitcast(I32))
+
+        tabw = keep.tile([P, T], I32, name="tabw", align_bytes=64)
+        wg = keep.tile([P, 2, 2 * R], U8, name="wg", align_bytes=64)
+        wu = keep.tile([P, 2, R], I32, name="wu", align_bytes=64)
+        wd = keep.tile([P, N], I32, name="wd", align_bytes=64)
+        nc.sync.dma_start(tabw[:], tab_words[0].rearrange("p t b -> p (t b)").bitcast(I32))
+        nc.sync.dma_start(wu[:], wu_words.rearrange("a p n i -> p a (n i)").bitcast(I32))
+        nc.sync.dma_start(wg[:].bitcast(I32), wg_words.rearrange("a p n -> p a n").bitcast(I32))
+        nc.sync.dma_start(wd[:], wd_words[0].rearrange("p n i -> p (n i)").bitcast(I32))
+        nc.scalar.dma_start(tsc[0:P:4].bitcast(I32), tab_scales.rearrange("a q t -> (a q) t").bitcast(I32))
+        load_scales(nc.scalar, gsc, wg_scales)
+        load_scales(nc.gpsimd, usc, wu_scales)
+        for q in range(4):
+            nc.gpsimd.dma_start(dsc[32 * q : 32 * q + 4].bitcast(I32), wd_scales[0, 4 * q : 4 * q + 4, :].bitcast(I32))
+        r_rows = rT.rearrange("(p t) c -> p t c", t=4)
+        res = []
+        for t in range(4):
+            window = keep.tile([P, T], F32, name=f"res{t}", align_bytes=64)
+            nc.sync.dma_start(window[:], r_rows[:, t, :])
+            res.append(window)
+
+        ident = keep.tile([P, P], F32, name="ident")
+        make_identity(nc, ident[:])
+
+        picked_sc = keep.tile([P, J], U8, name="picked_sc", align_bytes=64)
+        nc.vector.tensor_copy(picked_sc[:], tsc[:].indirect(offsets[:]))
+        for a in range(2):
+            for q in range(4):
+                first = 4 * (16 * a + 4 * q)
+                nc.scalar.dma_start(vsc[32 * q : 32 * q + 4, a, :].bitcast(I32), picked_sc[first : first + 16 : 4].bitcast(I32))
+        parted = []
+        for hf in range(2):
+            picked = keep.tile([P, HALF], U32, name="picked", align_bytes=64)
+            nc.vector.tensor_copy(picked[:], tabw[:].bitcast(U32).indirect(cols(hf * HALF, HALF)))
+            words = keep.tile([P, 4 * HALF], U8, name=f"parted{hf}", align_bytes=64)
+            nc.vector.tensor_copy(
+                words[:].bitcast(U16).rearrange("p (d c i) -> p c d i", d=2, i=8),
+                picked[:].bitcast(U16).rearrange("p (c i d) -> p c d i", d=2, i=8),
+            )
+            parted.append(words)
+
+        wd_dealt = keep.tile([P, N], I32, name="wd_dealt", align_bytes=64)
+        dsc_dealt = keep.tile([P, N], U8, name="dsc_dealt", align_bytes=64)
+        nc.vector.tensor_copy(wd_dealt[:].rearrange("p (t c i) -> p c t i", t=4, i=4),
+                              wd[:].rearrange("p (c i t) -> p c t i", t=4, i=4))
+        nc.vector.tensor_copy(dsc_dealt[:].rearrange("p (t c i) -> p c t i", t=4, i=16),
+                              dsc[:].rearrange("p (c i t) -> p c t i", t=4, i=16))
+
+        out_rows = out_0.rearrange("(p t) j -> p t j", t=4)
+        woven = [keep.tile([P, TAIL, 4], BF16, name=f"woven{c}", align_bytes=64) for c in range(4)]
+        o_codes = keep.tile([P, J], I32, name="o_codes", align_bytes=64)
+        o_scales = keep.tile([P, J], U8, name="o_scales", align_bytes=64)
+        y_rows = []
+
+        def first_stage(jt):
+            hf, j0 = jt // 4, (jt % 4) * P
+            ga = psum.tile([P, R], F32, name="ga")
+            ub = psum.tile([P, R], F32, name="ub", bufs=3)
+            for acc, w, wsc in ((ga, lambda a: wg[:, a, :].bitcast(FP4X4), gsc), (ub, lambda a: wu[:, a, :].bitcast(FP8X4), usc)):
+                for a in range(2):
+                    b0 = 2 * (a * HALF + j0)
+                    nc.tensor.matmul_mx(
+                        out=acc[:], lhsT=parted[hf][:, b0 : b0 + 2 * P].bitcast(FP4X4),
+                        lhsT_scale=vsc[:, a, jt * P : (jt + 1) * P],
+                        rhs=w(a), rhs_scale=wsc[:, a, :], start=(a == 0), stop=(a == 1))
+            gate = ring.tile([P, R], F32, name="gate", align_bytes=64)
+            nc.scalar.activation(gate[:].rearrange("j (u p e) -> j u p e", u=2, e=2),
+                                 ga[:].rearrange("j (p u e) -> j u p e", u=2, e=2), SIGMOID)
+            h_rows = ring.tile([P, R], BF16, name="h_rows", align_bytes=64)
+            nc.vector.tensor_tensor(h_rows[:].rearrange("j (u p e) -> j u p e", u=2, e=2),
+                                    ub[:].rearrange("j (p u e) -> j u p e", u=2, e=2),
+                                    gate[:].rearrange("j (u p e) -> j u p e", u=2, e=2), MULT)
+            return h_rows
+
+        def second_stage(pair, c):
+            turned = psum.tile([P, 2, 2, P], F32, name="turned", bufs=1)
+            for s in range(2):
+                for u in range(2):
+                    nc.tensor.transpose(turned[:, s, u, :], pair[s][:].bitcast(F32)[:, u * P : (u + 1) * P], ident[:])
+            h_woven = ring.tile([P, 4 * TAIL], BF16, name="h_woven", align_bytes=64)
+            nc.scalar.copy(h_woven[:].bitcast(F32).rearrange("p (s j u) -> p s j u", s=2, u=2),
+                           turned[:].rearrange("p s u j -> p s j u"))
+            h_codes = ring.tile([P, TAIL], I32, name="h_codes", align_bytes=64)
+            h_scales = ring.tile([P, TAIL], U8, name="h_scales", align_bytes=64)
+            nc.vector.quantize_mx(out=h_codes[:].bitcast(FP8X4), scales=h_scales[:], in_=h_woven[:])
+            rows = keep.tile([P, 4, TAIL], F32, name=f"y_rows{c}", align_bytes=64)
+            for u in range(2):
+                y = psum.tile([P, 2, TAIL], F32, name="y")
+                for t in (2 * u, 2 * u + 1):
+                    nc.tensor.matmul_mx(out=y[:, t % 2, :], lhsT=wd_dealt[:, t * P : (t + 1) * P].bitcast(FP8X4),
+                                        lhsT_scale=dsc_dealt[:, t * P : (t + 1) * P],
+                                        rhs=h_codes[:].bitcast(FP8X4), rhs_scale=h_scales[:], start=True, stop=True)
+                nc.scalar.copy(rows[:, 2 * u : 2 * u + 2, :], y[:])
+            y_rows.append(rows)
+
+        pairs = []
+        for b in range(4):
+            pairs.append([first_stage(2 * b + s) for s in range(2)])
+            if b > 0:
+                second_stage(pairs[b - 1], b - 1)
+        second_stage(pairs[3], 3)
+
+        low = [keep.tile([P, 2, HALF], F32, name=f"low{hf}", align_bytes=64) for hf in range(2)]
+        high = [keep.tile([P, 2, TAIL], F32, name=f"high{c}", align_bytes=64) for c in range(4)]
+        early = {}
+
+        def weave(pair_tile, u, c, j0):
+            nc.scalar.copy(woven[c][:, :, 2 * u : 2 * u + 2], pair_tile[:, :, j0 : j0 + TAIL].rearrange("p t j -> p j t"))
+
+        def gather(t, hf):
+            early[t, hf] = keep.tile([P, HALF], F32, name=f"early{t}{hf}", align_bytes=64)
+            nc.vector.tensor_copy(early[t, hf][:], res[t][:].indirect(cols(hf * HALF, HALF)))
+
+        def finish(t, c):
+            hf, j0 = divmod(c * TAIL, HALF)
+            span = slice(c * TAIL, (c + 1) * TAIL)
+            dst = low[hf][:, t, j0 : j0 + TAIL] if t < 2 else high[c][:, t - 2, :]
+            if (t, hf) in early:
+                nc.vector.tensor_tensor(dst, y_rows[c][:, t, :], early[t, hf][:, j0 : j0 + TAIL], ADD)
+            else:
+                nc.vector.tensor_tensor(dst, res[t][:].indirect(cols(c * TAIL, TAIL)), y_rows[c][:, t, :], ADD)
+            if t == 1:
+                weave(low[hf], 0, c, j0)
+                if c % 2 == 1:
+                    nc.sync.dma_start(out_rows[:, 0:2, hf * HALF : (hf + 1) * HALF], low[hf][:])
+            if t == 3:
+                nc.sync.dma_start(out_rows[:, 2:4, span], high[c][:])
+                weave(high[c], 1, c, 0)
+                nc.vector.quantize_mx(out=o_codes[:, span].bitcast(FP8X4), scales=o_scales[:, span],
+                                      in_=woven[c][:].rearrange("p j t -> p (j t)"))
+
+        gather(0, 0)
+        gather(0, 1)
+        finish(0, 0)
+        finish(0, 1)
+        finish(1, 0)
+        finish(1, 1)
+        gather(1, 1)
+        finish(0, 2)
+        finish(1, 2)
+        finish(0, 3)
+        finish(1, 3)
+        for t in (2, 3):
+            for c in range(4):
+                finish(t, c)
+
+        code_rows = out_1[0].rearrange("p j b -> p (j b)").bitcast(I32)
+        for hf in range(2):
+            nc.sync.dma_start(code_rows[:, hf * HALF : (hf + 1) * HALF], o_codes[:, hf * HALF : (hf + 1) * HALF])
+        for q in range(4):
+            (nc.sync if q % 2 == 0 else nc.scalar).dma_start(out_2[0, 4 * q : 4 * q + 4, :].bitcast(I32), o_scales[32 * q : 32 * q + 4].bitcast(I32))

@@ -40,71 +40,83 @@ def tile_list_gmlpt_sigm_resLP_kernel(
             return offsets[:, first // 16 : (first + count) // 16]
 
 
-        tsc = keep.tile([P, T], U8, name="tsc", align_bytes=64)
+        shared = ctx.enter_context(tc.tile_pool(name="shared", bufs=1))
+        KB = 1024
+        tsc = shared.tile([P, T], U8, name="tsc", align_bytes=64, offset=15 * KB + 512)
         gsc = keep.tile([P, 2, R], U8, name="gsc", align_bytes=64)
         usc = keep.tile([P, 2, R], U8, name="usc", align_bytes=64)
-        dsc = keep.tile([P, N], U8, name="dsc", align_bytes=64)
         vsc = keep.tile([P, 2, J], U8, name="vsc", align_bytes=64)
+        nc.sync.dma_start(tsc[0:32].bitcast(I32), tab_scales.rearrange("a q t -> (a q) t").bitcast(I32))
+        nc.gpsimd.memset(gsc[:].bitcast(I32), 0)
         nc.gpsimd.memset(usc[:].bitcast(I32), 0)
-        nc.vector.memset(tsc[:].bitcast(I32), 0)
-        nc.vector.memset(gsc[:].bitcast(I32), 0)
-        nc.vector.memset(dsc[:].bitcast(I32), 0)
-        nc.vector.memset(vsc[:].bitcast(I32), 0)
+        nc.gpsimd.memset(vsc[:].bitcast(I32), 0)
+        nc.vector.memset(tsc[32:64].bitcast(I32), 0)
+        nc.vector.memset(tsc[64:128].bitcast(I32), 0)
 
         def load_scales(queue, tile, dram):
             for q in range(4):
                 queue.dma_start(tile[32 * q : 32 * q + 4].bitcast(I32),
                                 dram[:, 4 * q : 4 * q + 4, :].rearrange("a r n -> r a n").bitcast(I32))
 
-        tabw = keep.tile([P, T], I32, name="tabw", align_bytes=64)
+        tabw = shared.tile([P, T], I32, name="tabw", align_bytes=64, offset=33 * KB)
         wg = keep.tile([P, 2, 2 * R], U8, name="wg", align_bytes=64)
-        wu = keep.tile([P, 2, R], I32, name="wu", align_bytes=64)
-        wd = keep.tile([P, N], I32, name="wd", align_bytes=64)
-        nc.sync.dma_start(tabw[:], tab_words[0].rearrange("p t b -> p (t b)").bitcast(I32))
-        nc.sync.dma_start(wu[:], wu_words.rearrange("a p n i -> p a (n i)").bitcast(I32))
+        load_scales(nc.sync, gsc, wg_scales)
         nc.sync.dma_start(wg[:].bitcast(I32), wg_words.rearrange("a p n -> p a n").bitcast(I32))
-        nc.sync.dma_start(wd[:], wd_words[0].rearrange("p n i -> p (n i)").bitcast(I32))
-        nc.scalar.dma_start(tsc[0:P:4].bitcast(I32), tab_scales.rearrange("a q t -> (a q) t").bitcast(I32))
-        load_scales(nc.scalar, gsc, wg_scales)
+        nc.sync.dma_start(tabw[:], tab_words[0].rearrange("p t b -> p (t b)").bitcast(I32))
         load_scales(nc.gpsimd, usc, wu_scales)
-        for q in range(4):
-            nc.gpsimd.dma_start(dsc[32 * q : 32 * q + 4].bitcast(I32), wd_scales[0, 4 * q : 4 * q + 4, :].bitcast(I32))
-        r_rows = rT.rearrange("(p t) c -> p t c", t=4)
-        res = []
-        for t in range(4):
-            window = keep.tile([P, T], F32, name=f"res{t}", align_bytes=64)
-            nc.sync.dma_start(window[:], r_rows[:, t, :])
-            res.append(window)
 
-        ident = keep.tile([P, P], F32, name="ident")
-        make_identity(nc, ident[:])
 
         picked_sc = keep.tile([P, J], U8, name="picked_sc", align_bytes=64)
         nc.vector.tensor_copy(picked_sc[:], tsc[:].indirect(offsets[:]))
-        for a in range(2):
-            for q in range(4):
-                first = 4 * (16 * a + 4 * q)
-                nc.scalar.dma_start(vsc[32 * q : 32 * q + 4, a, :].bitcast(I32), picked_sc[first : first + 16 : 4].bitcast(I32))
+        r_rows = rT.rearrange("(p t) c -> p t c", t=4)
+        res = []
+
+        def load_res(t, place):
+            window = shared.tile([P, T], F32, name=f"res{t}", align_bytes=64, offset=int(place * KB))
+            nc.sync.dma_start(window[:], r_rows[:, t, :])
+            res.append(window)
+
+        def move(m, queue):
+            a, q = divmod(m, 4)
+            queue.dma_start(vsc[32 * q : 32 * q + 4, a, :].bitcast(I32), picked_sc[4 * m : 4 * m + 4].bitcast(I32))
+
+        wu = shared.tile([P, 2, R], I32, name="wu", align_bytes=64, offset=19 * KB)
+        wd = shared.tile([P, N], I32, name="wd", align_bytes=64, offset=16 * KB)
+        dsc = shared.tile([P, N], U8, name="dsc", align_bytes=64, offset=18 * KB)
+        nc.sync.dma_start(wu[:], wu_words.rearrange("a p n i -> p a (n i)").bitcast(I32))
+        nc.vector.tensor_copy(vsc[0:32, 0, :].bitcast(I32), picked_sc[0:32].bitcast(I32))
+        nc.vector.memset(dsc[:].bitcast(I32), 0)
+        for m in (4, 5, 6, 7, 1, 2, 3):
+            move(m, nc.sync)
+        nc.sync.dma_start(wd[:], wd_words[0].rearrange("p n i -> p (n i)").bitcast(I32))
+        for q in range(4):
+            nc.sync.dma_start(dsc[32 * q : 32 * q + 4].bitcast(I32), wd_scales[0, 4 * q : 4 * q + 4, :].bitcast(I32))
+        load_res(0, 0)
+        ident = keep.tile([P, P], F32, name="ident")
+        make_identity(nc, ident[:])
         parted = []
         for hf in range(2):
-            picked = keep.tile([P, HALF], U32, name="picked", align_bytes=64)
+            picked = shared.tile([P, HALF], U32, name=f"picked{hf}", align_bytes=64, offset=58 * KB)
             nc.vector.tensor_copy(picked[:], tabw[:].bitcast(U32).indirect(cols(hf * HALF, HALF)))
             words = keep.tile([P, 4 * HALF], U8, name=f"parted{hf}", align_bytes=64)
-            nc.vector.tensor_copy(
-                words[:].bitcast(U16).rearrange("p (d c i) -> p c d i", d=2, i=8),
-                picked[:].bitcast(U16).rearrange("p (c i d) -> p c d i", d=2, i=8),
-            )
+            for c0, c1 in ((0, 16), (16, 64)) if hf == 0 else ((0, 64),):
+                nc.vector.tensor_copy(
+                    words[:].bitcast(U16).rearrange("p (d c i) -> p c d i", d=2, i=8)[:, c0:c1],
+                    picked[:].bitcast(U16).rearrange("p (c i d) -> p c d i", d=2, i=8)[:, c0:c1],
+                )
             parted.append(words)
+        load_res(1, 25)
+        load_res(2, 41)
+        load_res(3, 59.5)
 
-        wd_dealt = keep.tile([P, N], I32, name="wd_dealt", align_bytes=64)
-        dsc_dealt = keep.tile([P, N], U8, name="dsc_dealt", align_bytes=64)
+        wd_dealt = shared.tile([P, N], I32, name="wd_dealt", align_bytes=64, offset=57 * KB)
+        dsc_dealt = shared.tile([P, N], U8, name="dsc_dealt", align_bytes=64, offset=59 * KB)
         nc.vector.tensor_copy(wd_dealt[:].rearrange("p (t c i) -> p c t i", t=4, i=4),
                               wd[:].rearrange("p (c i t) -> p c t i", t=4, i=4))
         nc.vector.tensor_copy(dsc_dealt[:].rearrange("p (t c i) -> p c t i", t=4, i=16),
                               dsc[:].rearrange("p (c i t) -> p c t i", t=4, i=16))
 
         out_rows = out_0.rearrange("(p t) j -> p t j", t=4)
-        woven = [keep.tile([P, TAIL, 4], BF16, name=f"woven{c}", align_bytes=64) for c in range(4)]
         o_codes = keep.tile([P, J], I32, name="o_codes", align_bytes=64)
         o_scales = keep.tile([P, J], U8, name="o_scales", align_bytes=64)
         y_rows = []
@@ -120,7 +132,7 @@ def tile_list_gmlpt_sigm_resLP_kernel(
                         out=acc[:], lhsT=parted[hf][:, b0 : b0 + 2 * P].bitcast(FP4X4),
                         lhsT_scale=vsc[:, a, jt * P : (jt + 1) * P],
                         rhs=w(a), rhs_scale=wsc[:, a, :], start=(a == 0), stop=(a == 1))
-            gate = ring.tile([P, R], F32, name="gate", align_bytes=64)
+            gate = keep.tile([P, R], F32, name=f"gate{jt}", tag=f"gate{jt}", align_bytes=64)
             nc.scalar.activation(gate[:].rearrange("j (u p e) -> j u p e", u=2, e=2),
                                  ga[:].rearrange("j (p u e) -> j u p e", u=2, e=2), SIGMOID)
             h_rows = ring.tile([P, R], BF16, name="h_rows", align_bytes=64)
@@ -129,18 +141,21 @@ def tile_list_gmlpt_sigm_resLP_kernel(
                                     gate[:].rearrange("j (u p e) -> j u p e", u=2, e=2), MULT)
             return h_rows
 
-        def second_stage(pair, c):
+        def turn(pair, c):
             turned = psum.tile([P, 2, 2, P], F32, name="turned", bufs=1)
             for s in range(2):
                 for u in range(2):
                     nc.tensor.transpose(turned[:, s, u, :], pair[s][:].bitcast(F32)[:, u * P : (u + 1) * P], ident[:])
-            h_woven = ring.tile([P, 4 * TAIL], BF16, name="h_woven", align_bytes=64)
+            h_woven = keep.tile([P, 4 * TAIL], BF16, name=f"h_woven{c}", tag=f"gate{8 + c}", align_bytes=64)
             nc.scalar.copy(h_woven[:].bitcast(F32).rearrange("p (s j u) -> p s j u", s=2, u=2),
                            turned[:].rearrange("p s u j -> p s j u"))
-            h_codes = ring.tile([P, TAIL], I32, name="h_codes", align_bytes=64)
+            h_codes = keep.tile([P, TAIL], I32, name=f"h_codes{c}", tag=f"gate{12 + c}", align_bytes=64)
             h_scales = ring.tile([P, TAIL], U8, name="h_scales", align_bytes=64)
             nc.vector.quantize_mx(out=h_codes[:].bitcast(FP8X4), scales=h_scales[:], in_=h_woven[:])
-            rows = keep.tile([P, 4, TAIL], F32, name=f"y_rows{c}", align_bytes=64)
+            return h_codes, h_scales
+
+        def second_stage(h_codes, h_scales, c):
+            rows = keep.tile([P, 4, TAIL], F32, name=f"y_rows{c}", tag=f"y_rows{c}", align_bytes=64)
             for u in range(2):
                 y = psum.tile([P, 2, TAIL], F32, name="y")
                 for t in (2 * u, 2 * u + 1):
@@ -150,57 +165,56 @@ def tile_list_gmlpt_sigm_resLP_kernel(
                 nc.scalar.copy(rows[:, 2 * u : 2 * u + 2, :], y[:])
             y_rows.append(rows)
 
-        pairs = []
-        for b in range(4):
-            pairs.append([first_stage(2 * b + s) for s in range(2)])
-            if b > 0:
-                second_stage(pairs[b - 1], b - 1)
-        second_stage(pairs[3], 3)
+        h_tiles = []
+        for jt in range(8):
+            h_tiles.append(first_stage(jt))
+            if jt >= 2 and jt % 2 == 0:
+                quantised = turn(h_tiles[jt - 2 : jt], jt // 2 - 1)
+            if jt >= 2 and jt % 2 == 1:
+                second_stage(*quantised, jt // 2 - 1)
+        second_stage(*turn(h_tiles[6:8], 3), 3)
 
-        low = [keep.tile([P, 2, HALF], F32, name=f"low{hf}", align_bytes=64) for hf in range(2)]
-        high = [keep.tile([P, 2, TAIL], F32, name=f"high{c}", align_bytes=64) for c in range(4)]
+        low = [keep.tile([P, 2, TAIL], F32, name=f"low{c}", align_bytes=64) for c in range(3)]
+        high = [keep.tile([P, 2, TAIL], F32, name=f"high{c}", tag=f"gate{(6, 7, 16)[c]}", align_bytes=64) for c in range(3)]
+        woven = [keep.tile([P, TAIL, 4], BF16, name=f"woven{c}", tag=f"gate{(9, 10, 11, 17)[c]}", align_bytes=64) for c in range(4)]
         early = {}
 
         def weave(pair_tile, u, c, j0):
             nc.scalar.copy(woven[c][:, :, 2 * u : 2 * u + 2], pair_tile[:, :, j0 : j0 + TAIL].rearrange("p t j -> p j t"))
 
-        def gather(t, hf):
-            early[t, hf] = keep.tile([P, HALF], F32, name=f"early{t}{hf}", align_bytes=64)
+        def gather(t, hf, after):
+            early[t, hf] = keep.tile([P, HALF], F32, name=f"early{t}{hf}", tag=f"gate{after}", align_bytes=64)
             nc.vector.tensor_copy(early[t, hf][:], res[t][:].indirect(cols(hf * HALF, HALF)))
 
         def finish(t, c):
             hf, j0 = divmod(c * TAIL, HALF)
             span = slice(c * TAIL, (c + 1) * TAIL)
-            dst = low[hf][:, t, j0 : j0 + TAIL] if t < 2 else high[c][:, t - 2, :]
+            pair = (low, high)[t // 2][c]
             if (t, hf) in early:
-                nc.vector.tensor_tensor(dst, y_rows[c][:, t, :], early[t, hf][:, j0 : j0 + TAIL], ADD)
+                nc.vector.tensor_tensor(pair[:, t % 2, :], y_rows[c][:, t, :], early[t, hf][:, j0 : j0 + TAIL], ADD)
             else:
-                nc.vector.tensor_tensor(dst, res[t][:].indirect(cols(c * TAIL, TAIL)), y_rows[c][:, t, :], ADD)
-            if t == 1:
-                weave(low[hf], 0, c, j0)
-                if c % 2 == 1:
-                    nc.sync.dma_start(out_rows[:, 0:2, hf * HALF : (hf + 1) * HALF], low[hf][:])
-            if t == 3:
-                nc.sync.dma_start(out_rows[:, 2:4, span], high[c][:])
-                weave(high[c], 1, c, 0)
-                nc.vector.quantize_mx(out=o_codes[:, span].bitcast(FP8X4), scales=o_scales[:, span],
-                                      in_=woven[c][:].rearrange("p j t -> p (j t)"))
+                nc.vector.tensor_tensor(pair[:, t % 2, :], res[t][:].indirect(cols(c * TAIL, TAIL)), y_rows[c][:, t, :], ADD)
+            if t % 2 == 1:
+                weave(pair, t // 2, c, 0)
+                nc.sync.dma_start(out_rows[:, t - 1 : t + 1, span], pair[:])
 
-        gather(0, 0)
-        gather(0, 1)
-        finish(0, 0)
-        finish(0, 1)
-        finish(1, 0)
-        finish(1, 1)
-        gather(1, 1)
-        finish(0, 2)
-        finish(1, 2)
-        finish(0, 3)
-        finish(1, 3)
-        for t in (2, 3):
-            for c in range(4):
+        for t, hf, after in ((0, 0, 2), (0, 1, 3)):
+            gather(t, hf, after)
+        for c in range(3):
+            for t in range(3):
                 finish(t, c)
+        for c in range(3):
+            finish(3, c)
+        last = keep.tile([P, 4, TAIL], F32, name="last", tag="y_rows2", align_bytes=64)
+        low.append(last[:, 0:2, :])
+        high.append(last[:, 2:4, :])
+        for t in range(4):
+            finish(t, 3)
 
+        for c in range(4):
+            span = slice(c * TAIL, (c + 1) * TAIL)
+            nc.vector.quantize_mx(out=o_codes[:, span].bitcast(FP8X4), scales=o_scales[:, span],
+                                  in_=woven[c][:].rearrange("p j t -> p (j t)"))
         code_rows = out_1[0].rearrange("p j b -> p (j b)").bitcast(I32)
         for hf in range(2):
             nc.sync.dma_start(code_rows[:, hf * HALF : (hf + 1) * HALF], o_codes[:, hf * HALF : (hf + 1) * HALF])

@@ -63,7 +63,7 @@ def tile_list_gmlpt_sigm_resLP_kernel(
         load_scales(nc.sync, gsc, wg_scales)
         nc.sync.dma_start(wg[:].bitcast(I32), wg_words.rearrange("a p n -> p a n").bitcast(I32))
         nc.sync.dma_start(tabw[:], tab_words[0].rearrange("p t b -> p (t b)").bitcast(I32))
-        load_scales(nc.gpsimd, usc, wu_scales)
+        load_scales(nc.sync, usc, wu_scales)
 
 
         picked_sc = keep.tile([P, J], U8, name="picked_sc", align_bytes=64)

@@ -1,7 +1,6 @@
 from contextlib import ExitStack
 
 import concourse.mybir as mybir
-from concourse.masks import make_identity
 
 K, R, N, T, J = 1024, 512, 512, 4096, 1024
 FLOPS = 2 * J * (2 * K * R + R * N)
@@ -20,7 +19,8 @@ SIGMOID = mybir.ActivationFunctionType.Sigmoid
 
 P = 128
 HALF = 512
-TAIL = 256
+QUARTER = 256
+KB = 1024
 
 
 def tile_list_gmlpt_sigm_resLP_kernel(
@@ -32,6 +32,7 @@ def tile_list_gmlpt_sigm_resLP_kernel(
         keep = ctx.enter_context(tc.tile_pool(name="keep", bufs=1))
         ring = ctx.enter_context(tc.tile_pool(name="ring", bufs=4))
         psum = ctx.enter_context(tc.psum_pool(name="psum", bufs=2))
+        shared = ctx.enter_context(tc.tile_pool(name="shared", bufs=1))
 
         offsets = keep.tile([P, J // 16], U16, name="offsets")
         nc.sync.dma_start(offsets[:], offs)
@@ -39,184 +40,181 @@ def tile_list_gmlpt_sigm_resLP_kernel(
         def cols(first, count):
             return offsets[:, first // 16 : (first + count) // 16]
 
+        tsc = keep.tile([P, T], U8, name="tsc", align_bytes=64)
+        wsc = keep.tile([P, 3 * R], U8, name="wsc", align_bytes=64)
+        staged = keep.tile([P, J + 3 * R], U8, name="staged", align_bytes=64)
+        both = keep.tile([P, 2, J + 3 * R], U8, name="both", align_bytes=64)
+        plane0, plane1 = both[:, 0, :], both[:, 1, :]
+        nc.vector.memset(wsc[:, 2 * R : 3 * R].bitcast(I32), 0)
+        nc.sync.dma_start(tsc[0:32].bitcast(I32), tab_scales.rearrange("a q t -> q a t").bitcast(I32))
+        nc.sync.dma_start(wsc[0:32, 0:R].bitcast(I32), wg_scales.rearrange("a q n -> q a n").bitcast(I32))
+        nc.sync.dma_start(wsc[0:32, R : 2 * R].bitcast(I32), wu_scales.rearrange("a q n -> q a n").bitcast(I32))
+        nc.sync.dma_start(wsc[0:32:2, 2 * R : 3 * R].bitcast(I32), wd_scales[0].bitcast(I32))
+        for rows in (slice(32, 64), slice(64, 128)):
+            nc.gpsimd.memset(wsc[rows, 0 : 2 * R].bitcast(I32), 0)
+            nc.vector.memset(tsc[rows].bitcast(I32), 0)
+        nc.gpsimd.memset(both[:].bitcast(I32), 0)
 
-        shared = ctx.enter_context(tc.tile_pool(name="shared", bufs=1))
-        KB = 1024
-        tsc = shared.tile([P, T], U8, name="tsc", align_bytes=64, offset=15 * KB + 512)
-        gsc = keep.tile([P, 2, R], U8, name="gsc", align_bytes=64)
-        usc = keep.tile([P, 2, R], U8, name="usc", align_bytes=64)
-        vsc = keep.tile([P, 2, J], U8, name="vsc", align_bytes=64)
-        nc.sync.dma_start(tsc[0:32].bitcast(I32), tab_scales.rearrange("a q t -> (a q) t").bitcast(I32))
-        nc.gpsimd.memset(gsc[:].bitcast(I32), 0)
-        nc.gpsimd.memset(usc[:].bitcast(I32), 0)
-        nc.gpsimd.memset(vsc[:].bitcast(I32), 0)
-        nc.vector.memset(tsc[32:64].bitcast(I32), 0)
-        nc.vector.memset(tsc[64:128].bitcast(I32), 0)
-
-        def load_scales(queue, tile, dram):
-            for q in range(4):
-                queue.dma_start(tile[32 * q : 32 * q + 4].bitcast(I32),
-                                dram[:, 4 * q : 4 * q + 4, :].rearrange("a r n -> r a n").bitcast(I32))
-
-        tabw = shared.tile([P, T], I32, name="tabw", align_bytes=64, offset=33 * KB)
-        wg = keep.tile([P, 2, 2 * R], U8, name="wg", align_bytes=64)
-        load_scales(nc.sync, gsc, wg_scales)
-        nc.sync.dma_start(wg[:].bitcast(I32), wg_words.rearrange("a p n -> p a n").bitcast(I32))
+        wg = shared.tile([P, 70 * KB], U8, name="wg", align_bytes=64, offset=0)
+        tabw = keep.tile([P, T], I32, name="tabw", align_bytes=64)
+        nc.sync.dma_start(wg[:, 0 : 4 * R].bitcast(I32).rearrange("p (a n) -> p a n", a=2),
+                          wg_words.rearrange("a p n -> p a n").bitcast(I32))
         nc.sync.dma_start(tabw[:], tab_words[0].rearrange("p t b -> p (t b)").bitcast(I32))
-        load_scales(nc.sync, usc, wu_scales)
+        wu = keep.tile([P, 2 * R], I32, name="wu", align_bytes=64)
+        nc.sync.dma_start(wu[:].rearrange("p (a n) -> p a n", a=2), wu_words.rearrange("a p n i -> p a (n i)").bitcast(I32))
 
-
-        picked_sc = keep.tile([P, J], U8, name="picked_sc", align_bytes=64)
+        nc.gpsimd.tensor_copy(staged[:, J:].rearrange("p (w t c i) -> p w c t i", w=3, t=4, i=16),
+                              wsc[:].rearrange("p (w c i t) -> p w c t i", w=3, t=4, i=16))
+        picked_sc = shared.tile([P, J], U8, name="picked_sc", align_bytes=64, offset=70 * KB)
         nc.vector.tensor_copy(picked_sc[:], tsc[:].indirect(offsets[:]))
+        nc.vector.tensor_copy(staged[0:32, 0:J].bitcast(I32), picked_sc[0:32].bitcast(I32))
+        for q in (0, 2, 1, 3):
+            nc.sync.dma_start(both[32 * q : 32 * q + 4].bitcast(I32), staged[8 * q : 8 * q + 8].bitcast(I32))
+
+        wg_dealt = shared.tile([P, 4 * R], U8, name="wg_dealt", align_bytes=64, offset=70 * KB)
+        nc.vector.tensor_copy(wg_dealt[:].bitcast(U16).rearrange("p (a t c i) -> p a c t i", a=2, t=4, i=8),
+                              wg[:, 0 : 4 * R].bitcast(U16).rearrange("p (a c i t) -> p a c t i", a=2, t=4, i=8))
+
+        warm = psum.tile([P, R], F32, name="warm", tag="y", bufs=3)
+        for w in range(4):
+            early = wg_dealt[:, 0 : 2 * P].bitcast(FP4X4) if w < 2 else wu[:, 0:P].bitcast(FP8X4)
+            nc.tensor.matmul_mx(out=warm[:], lhsT=early, lhsT_scale=wsc[:, 0:P],
+                                rhs=wg_dealt[:, 0 : 2 * R].bitcast(FP4X4), rhs_scale=wsc[:, 0:R], start=True, stop=True)
+        wd = shared.tile([P, N], I32, name="wd", align_bytes=64, offset=4 * KB)
+        nc.sync.dma_start(wd[:], wd_words[0].rearrange("p n i -> p (n i)").bitcast(I32))
         r_rows = rT.rearrange("(p t) c -> p t c", t=4)
         res = []
-
-        def load_res(t, place):
-            window = shared.tile([P, T], F32, name=f"res{t}", align_bytes=64, offset=int(place * KB))
+        for t in range(4):
+            window = shared.tile([P, T], F32, name=f"res{t}", align_bytes=64, offset=(6 + 16 * t) * KB)
             nc.sync.dma_start(window[:], r_rows[:, t, :])
             res.append(window)
 
-        def move(m, queue):
-            a, q = divmod(m, 4)
-            queue.dma_start(vsc[32 * q : 32 * q + 4, a, :].bitcast(I32), picked_sc[4 * m : 4 * m + 4].bitcast(I32))
-
-        wu = shared.tile([P, 2, R], I32, name="wu", align_bytes=64, offset=19 * KB)
-        wd = shared.tile([P, N], I32, name="wd", align_bytes=64, offset=16 * KB)
-        dsc = shared.tile([P, N], U8, name="dsc", align_bytes=64, offset=18 * KB)
-        nc.sync.dma_start(wu[:], wu_words.rearrange("a p n i -> p a (n i)").bitcast(I32))
-        nc.vector.tensor_copy(vsc[0:32, 0, :].bitcast(I32), picked_sc[0:32].bitcast(I32))
-        nc.vector.memset(dsc[:].bitcast(I32), 0)
-        for m in (4, 5, 6, 7, 1, 2, 3):
-            move(m, nc.sync)
-        nc.sync.dma_start(wd[:], wd_words[0].rearrange("p n i -> p (n i)").bitcast(I32))
-        for q in range(4):
-            nc.sync.dma_start(dsc[32 * q : 32 * q + 4].bitcast(I32), wd_scales[0, 4 * q : 4 * q + 4, :].bitcast(I32))
-        load_res(0, 0)
-        ident = keep.tile([P, P], F32, name="ident")
-        make_identity(nc, ident[:])
         parted = []
-        for hf in range(2):
-            picked = shared.tile([P, HALF], U32, name=f"picked{hf}", align_bytes=64, offset=58 * KB)
+
+        def pick_words(hf):
+            picked = shared.tile([P, HALF], U32, name=f"picked{hf}", align_bytes=64, offset=(96 + hf) * KB)
             nc.vector.tensor_copy(picked[:], tabw[:].bitcast(U32).indirect(cols(hf * HALF, HALF)))
             words = keep.tile([P, 4 * HALF], U8, name=f"parted{hf}", align_bytes=64)
-            for c0, c1 in ((0, 16), (16, 64)) if hf == 0 else ((0, 64),):
-                nc.vector.tensor_copy(
-                    words[:].bitcast(U16).rearrange("p (d c i) -> p c d i", d=2, i=8)[:, c0:c1],
-                    picked[:].bitcast(U16).rearrange("p (c i d) -> p c d i", d=2, i=8)[:, c0:c1],
-                )
+            nc.vector.tensor_copy(
+                words[:].bitcast(U16).rearrange("p (d c i) -> p c d i", d=2, i=8),
+                picked[:].bitcast(U16).rearrange("p (c i d) -> p c d i", d=2, i=8),
+            )
             parted.append(words)
-        load_res(1, 25)
-        load_res(2, 41)
-        load_res(3, 59.5)
 
-        wd_dealt = shared.tile([P, N], I32, name="wd_dealt", align_bytes=64, offset=57 * KB)
-        dsc_dealt = shared.tile([P, N], U8, name="dsc_dealt", align_bytes=64, offset=59 * KB)
+        pick_words(0)
+        wu_dealt = shared.tile([P, 2 * R], I32, name="wu_dealt", align_bytes=64, offset=93 * KB)
+        nc.vector.tensor_copy(wu_dealt[:].rearrange("p (a t c i) -> p a c t i", a=2, t=4, i=4),
+                              wu[:].rearrange("p (a c i t) -> p a c t i", a=2, t=4, i=4))
+        pick_words(1)
+        wd_dealt = keep.tile([P, N], I32, name="wd_dealt", align_bytes=64)
         nc.vector.tensor_copy(wd_dealt[:].rearrange("p (t c i) -> p c t i", t=4, i=4),
                               wd[:].rearrange("p (c i t) -> p c t i", t=4, i=4))
-        nc.vector.tensor_copy(dsc_dealt[:].rearrange("p (t c i) -> p c t i", t=4, i=16),
-                              dsc[:].rearrange("p (c i t) -> p c t i", t=4, i=16))
 
-        out_rows = out_0.rearrange("(p t) j -> p t j", t=4)
-        o_codes = keep.tile([P, J], I32, name="o_codes", align_bytes=64)
-        o_scales = keep.tile([P, J], U8, name="o_scales", align_bytes=64)
-        y_rows = []
+        sums0 = keep.tile([P, 4, HALF], F32, name="sums0", align_bytes=64)
+        sums1 = keep.tile([P, 5 * HALF], F32, name="sums1", align_bytes=64)
+        sums = [sums0[:], sums1[:, 0 : 4 * HALF].rearrange("p (t j) -> p t j", t=4)]
+        planes = (plane0, plane1)
 
-        def first_stage(jt):
-            hf, j0 = jt // 4, (jt % 4) * P
-            ga = psum.tile([P, R], F32, name="ga")
-            ub = psum.tile([P, R], F32, name="ub", bufs=3)
-            for acc, w, wsc in ((ga, lambda a: wg[:, a, :].bitcast(FP4X4), gsc), (ub, lambda a: wu[:, a, :].bitcast(FP8X4), usc)):
+        def gates(c, gate):
+            hf, j0 = divmod(c * QUARTER, HALF)
+            for u in range(2):
+                ga = psum.tile([P, 2, QUARTER], F32, name="ga", bufs=3)
+                for e in range(2):
+                    t = 2 * u + e
+                    for a in range(2):
+                        c0 = a * R + t * P
+                        b0 = 2 * (a * HALF + j0)
+                        nc.tensor.matmul_mx(
+                            out=ga[:, e, :], lhsT=wg_dealt[:, 2 * c0 : 2 * (c0 + P)].bitcast(FP4X4),
+                            lhsT_scale=planes[a][:, J + t * P : J + (t + 1) * P],
+                            rhs=parted[hf][:, b0 : b0 + 2 * QUARTER].bitcast(FP4X4),
+                            rhs_scale=planes[a][:, c * QUARTER : (c + 1) * QUARTER], start=(a == 0), stop=(a == 1))
+                nc.scalar.activation(gate[:, u, :].rearrange("p (j e) -> p j e", e=2), ga[:].rearrange("p e j -> p j e"), SIGMOID)
+
+        def gated(jt, gate, h_out):
+            hf, j0 = divmod(jt * P, HALF)
+            ub = psum.tile([P, 4, P], F32, name="ub", bufs=2)
+            for t in range(4):
                 for a in range(2):
+                    c0 = a * R + t * P
+                    s0 = J + R + t * P
                     b0 = 2 * (a * HALF + j0)
                     nc.tensor.matmul_mx(
-                        out=acc[:], lhsT=parted[hf][:, b0 : b0 + 2 * P].bitcast(FP4X4),
-                        lhsT_scale=vsc[:, a, jt * P : (jt + 1) * P],
-                        rhs=w(a), rhs_scale=wsc[:, a, :], start=(a == 0), stop=(a == 1))
-            gate = keep.tile([P, R], F32, name=f"gate{jt}", tag=f"gate{jt}", align_bytes=64)
-            nc.scalar.activation(gate[:].rearrange("j (u p e) -> j u p e", u=2, e=2),
-                                 ga[:].rearrange("j (p u e) -> j u p e", u=2, e=2), SIGMOID)
-            h_rows = ring.tile([P, R], BF16, name="h_rows", align_bytes=64)
-            nc.vector.tensor_tensor(h_rows[:].rearrange("j (u p e) -> j u p e", u=2, e=2),
-                                    ub[:].rearrange("j (p u e) -> j u p e", u=2, e=2),
-                                    gate[:].rearrange("j (u p e) -> j u p e", u=2, e=2), MULT)
-            return h_rows
+                        out=ub[:, t, :], lhsT=wu_dealt[:, c0 : c0 + P].bitcast(FP8X4), lhsT_scale=planes[a][:, s0 : s0 + P],
+                        rhs=parted[hf][:, b0 : b0 + 2 * P].bitcast(FP4X4),
+                        rhs_scale=planes[a][:, jt * P : (jt + 1) * P], start=(a == 0), stop=(a == 1))
+            s = jt % 2
+            nc.vector.tensor_tensor(h_out.rearrange("p (j u e) -> p j u e", u=2, e=2),
+                                    ub[:].rearrange("p (u e) j -> p j u e", u=2),
+                                    gate[:, :, 2 * s * P : 2 * (s + 1) * P].rearrange("p u (j e) -> p j u e", e=2), MULT)
 
-        def turn(pair, c):
-            turned = psum.tile([P, 2, 2, P], F32, name="turned", bufs=1)
-            for s in range(2):
-                for u in range(2):
-                    nc.tensor.transpose(turned[:, s, u, :], pair[s][:].bitcast(F32)[:, u * P : (u + 1) * P], ident[:])
-            h_woven = keep.tile([P, 4 * TAIL], BF16, name=f"h_woven{c}", tag=f"gate{8 + c}", align_bytes=64)
-            nc.scalar.copy(h_woven[:].bitcast(F32).rearrange("p (s j u) -> p s j u", s=2, u=2),
-                           turned[:].rearrange("p s u j -> p s j u"))
-            h_codes = keep.tile([P, TAIL], I32, name=f"h_codes{c}", tag=f"gate{12 + c}", align_bytes=64)
-            h_scales = ring.tile([P, TAIL], U8, name="h_scales", align_bytes=64)
-            nc.vector.quantize_mx(out=h_codes[:].bitcast(FP8X4), scales=h_scales[:], in_=h_woven[:])
+        y_rows = {}
+
+        def quantise_h(h_woven):
+            h_codes = ring.tile([P, QUARTER], I32, name="h_codes", align_bytes=64)
+            h_scales = ring.tile([P, QUARTER], U8, name="h_scales", align_bytes=64)
+            nc.vector.quantize_mx(out=h_codes[:].bitcast(FP8X4), scales=h_scales[:], in_=h_woven)
             return h_codes, h_scales
 
-        def second_stage(h_codes, h_scales, c):
-            rows = keep.tile([P, 4, TAIL], F32, name=f"y_rows{c}", tag=f"y_rows{c}", align_bytes=64)
-            for u in range(2):
-                y = psum.tile([P, 2, TAIL], F32, name="y")
-                for t in (2 * u, 2 * u + 1):
-                    nc.tensor.matmul_mx(out=y[:, t % 2, :], lhsT=wd_dealt[:, t * P : (t + 1) * P].bitcast(FP8X4),
-                                        lhsT_scale=dsc_dealt[:, t * P : (t + 1) * P],
+        def second_stage(h_codes, h_scales, c, pairs):
+            for u in pairs:
+                y = psum.tile([P, 2, QUARTER], F32, name="y", bufs=3)
+                for e in range(2):
+                    t = 2 * u + e
+                    s0 = J + 2 * R + t * P
+                    nc.tensor.matmul_mx(out=y[:, e, :], lhsT=wd_dealt[:, t * P : (t + 1) * P].bitcast(FP8X4),
+                                        lhsT_scale=plane0[:, s0 : s0 + P],
                                         rhs=h_codes[:].bitcast(FP8X4), rhs_scale=h_scales[:], start=True, stop=True)
-                nc.scalar.copy(rows[:, 2 * u : 2 * u + 2, :], y[:])
-            y_rows.append(rows)
+                if (c, u) == (1, 1):
+                    rows = sums1[:, 768:2304].rearrange("p (e x) -> p e x", x=QUARTER)[:, 0:6:5, :]
+                elif (c, u) == (2, 1):
+                    rows = sums1[:, 256:2560].rearrange("p (e x) -> p e x", x=QUARTER)[:, 0:9:8, :]
+                else:
+                    rows = keep.tile([P, 2, QUARTER], F32, name=f"y_rows{c}{u}", align_bytes=64)[:]
+                nc.scalar.copy(rows, y[:])
+                y_rows[c, u] = rows
 
-        h_tiles = []
-        for jt in range(8):
-            h_tiles.append(first_stage(jt))
-            if jt >= 2 and jt % 2 == 0:
-                quantised = turn(h_tiles[jt - 2 : jt], jt // 2 - 1)
-            if jt >= 2 and jt % 2 == 1:
-                second_stage(*quantised, jt // 2 - 1)
-        second_stage(*turn(h_tiles[6:8], 3), 3)
+        out_rows = out_0.rearrange("(p t) j -> p t j", t=4)
+        woven = [keep.tile([P, QUARTER, 4], BF16, name=f"woven{c}", align_bytes=64)[:] for c in range(4)]
 
-        low = [keep.tile([P, 2, TAIL], F32, name=f"low{c}", align_bytes=64) for c in range(3)]
-        high = [keep.tile([P, 2, TAIL], F32, name=f"high{c}", tag=f"gate{(6, 7, 16)[c]}", align_bytes=64) for c in range(3)]
-        woven = [keep.tile([P, TAIL, 4], BF16, name=f"woven{c}", tag=f"gate{(9, 10, 11, 17)[c]}", align_bytes=64) for c in range(4)]
-        early = {}
+        def add_residual(dst, t, c):
+            nc.vector.tensor_tensor(dst, res[t][:].indirect(cols(c * QUARTER, QUARTER)), y_rows[c, t // 2][:, t % 2, :], ADD)
 
-        def weave(pair_tile, u, c, j0):
-            nc.scalar.copy(woven[c][:, :, 2 * u : 2 * u + 2], pair_tile[:, :, j0 : j0 + TAIL].rearrange("p t j -> p j t"))
-
-        def gather(t, hf, after):
-            early[t, hf] = keep.tile([P, HALF], F32, name=f"early{t}{hf}", tag=f"gate{after}", align_bytes=64)
-            nc.vector.tensor_copy(early[t, hf][:], res[t][:].indirect(cols(hf * HALF, HALF)))
-
-        def finish(t, c):
-            hf, j0 = divmod(c * TAIL, HALF)
-            span = slice(c * TAIL, (c + 1) * TAIL)
-            pair = (low, high)[t // 2][c]
-            if (t, hf) in early:
-                nc.vector.tensor_tensor(pair[:, t % 2, :], y_rows[c][:, t, :], early[t, hf][:, j0 : j0 + TAIL], ADD)
-            else:
-                nc.vector.tensor_tensor(pair[:, t % 2, :], res[t][:].indirect(cols(c * TAIL, TAIL)), y_rows[c][:, t, :], ADD)
-            if t % 2 == 1:
-                weave(pair, t // 2, c, 0)
-                nc.sync.dma_start(out_rows[:, t - 1 : t + 1, span], pair[:])
-
-        for t, hf, after in ((0, 0, 2), (0, 1, 3)):
-            gather(t, hf, after)
-        for c in range(3):
-            for t in range(3):
-                finish(t, c)
-        for c in range(3):
-            finish(3, c)
-        last = keep.tile([P, 4, TAIL], F32, name="last", tag="y_rows2", align_bytes=64)
-        low.append(last[:, 0:2, :])
-        high.append(last[:, 2:4, :])
-        for t in range(4):
-            finish(t, 3)
+        def cell(t, c):
+            hf, j0 = divmod(c * QUARTER, HALF)
+            add_residual(sums[hf][:, t, j0 : j0 + QUARTER], t, c)
+            if t == 3:
+                weave = nc.scalar.copy if c < 3 else nc.vector.tensor_copy
+                weave(woven[c].rearrange("p (c i) t -> p c t i", i=2),
+                      sums[hf][:, :, j0 : j0 + QUARTER].rearrange("p t (c i) -> p c t i", i=2))
+            if c % 2 == 1 and t > 0:
+                rows = slice(0, 2) if t == 1 else slice(t, t + 1)
+                nc.sync.dma_start(out_rows[:, rows, hf * HALF : (hf + 1) * HALF], sums[hf][:, rows, :])
 
         for c in range(4):
-            span = slice(c * TAIL, (c + 1) * TAIL)
-            nc.vector.quantize_mx(out=o_codes[:, span].bitcast(FP8X4), scales=o_scales[:, span],
-                                  in_=woven[c][:].rearrange("p j t -> p (j t)"))
+            h_woven = ring.tile([P, 4 * QUARTER], BF16, name="h_woven", align_bytes=64)[:]
+            gate = ring.tile([P, 2, HALF], F32, name="gate", align_bytes=64)[:]
+            gates(c, gate)
+            for s in range(2):
+                gated(2 * c + s, gate, h_woven[:, s * HALF : (s + 1) * HALF])
+            if c > 0:
+                second_stage(*quantised, c - 1, (0, 1))
+            quantised = quantise_h(h_woven)
+        second_stage(*quantised, 3, (0, 1))
+        for t, c in ((0, 0), (1, 0), (0, 1), (1, 1), (0, 2), (1, 2), (2, 0), (2, 1), (2, 2), (0, 3), (1, 3), (2, 3)):
+            cell(t, c)
+        for c in range(4):
+            cell(3, c)
+        o_codes = keep.tile([P, J], I32, name="o_codes", align_bytes=64)
+        o_scales = keep.tile([P, J], U8, name="o_scales", align_bytes=64)
         code_rows = out_1[0].rearrange("p j b -> p (j b)").bitcast(I32)
-        for hf in range(2):
-            nc.sync.dma_start(code_rows[:, hf * HALF : (hf + 1) * HALF], o_codes[:, hf * HALF : (hf + 1) * HALF])
+        for c in range(4):
+            span = slice(c * QUARTER, (c + 1) * QUARTER)
+            nc.vector.quantize_mx(out=o_codes[:, span].bitcast(FP8X4), scales=o_scales[:, span],
+                                  in_=woven[c].rearrange("p j t -> p (j t)"))
+            if c > 0:
+                done = slice(0, HALF) if c == 1 else span
+                nc.sync.dma_start(code_rows[:, done], o_codes[:, done])
         for q in range(4):
-            (nc.sync if q % 2 == 0 else nc.scalar).dma_start(out_2[0, 4 * q : 4 * q + 4, :].bitcast(I32), o_scales[32 * q : 32 * q + 4].bitcast(I32))
+            queue = nc.sync if q % 2 == 0 else nc.scalar
+            queue.dma_start(out_2[0, 4 * q : 4 * q + 4, :].bitcast(I32), o_scales[32 * q : 32 * q + 4].bitcast(I32))

@@ -20,7 +20,16 @@ SIGMOID = mybir.ActivationFunctionType.Sigmoid
 P = 128
 HALF = 512
 QUARTER = 256
+LAST = J // QUARTER - 1
 KB = 1024
+
+WG_SCALES, WU_SCALES, WD_SCALES, SCALE_ROW = J, J + R, J + 2 * R, J + 2 * R + N
+
+WD_AT = 4 * KB
+WINDOWS_AT = 6 * KB
+LANDING_BYTES = WINDOWS_AT + 4 * 4 * T
+WU_DEALT_AT = 93 * KB
+PICKED_AT = WU_DEALT_AT + 3 * KB
 
 
 def tile_list_gmlpt_sigm_resLP_kernel(
@@ -37,184 +46,184 @@ def tile_list_gmlpt_sigm_resLP_kernel(
         offsets = keep.tile([P, J // 16], U16, name="offsets")
         nc.sync.dma_start(offsets[:], offs)
 
-        def cols(first, count):
+        def listed(first, count):
             return offsets[:, first // 16 : (first + count) // 16]
 
-        tsc = keep.tile([P, T], U8, name="tsc", align_bytes=64)
-        wsc = keep.tile([P, 3 * R], U8, name="wsc", align_bytes=64)
-        staged = keep.tile([P, J + 3 * R], U8, name="staged", align_bytes=64)
-        both = keep.tile([P, 2, J + 3 * R], U8, name="both", align_bytes=64)
-        plane0, plane1 = both[:, 0, :], both[:, 1, :]
-        nc.vector.memset(wsc[:, 2 * R : 3 * R].bitcast(I32), 0)
-        nc.sync.dma_start(tsc[0:32].bitcast(I32), tab_scales.rearrange("a q t -> q a t").bitcast(I32))
-        nc.sync.dma_start(wsc[0:32, 0:R].bitcast(I32), wg_scales.rearrange("a q n -> q a n").bitcast(I32))
-        nc.sync.dma_start(wsc[0:32, R : 2 * R].bitcast(I32), wu_scales.rearrange("a q n -> q a n").bitcast(I32))
-        nc.sync.dma_start(wsc[0:32:2, 2 * R : 3 * R].bitcast(I32), wd_scales[0].bitcast(I32))
+        table_rows = keep.tile([P, T], U8, name="table_rows", align_bytes=64)
+        weight_rows = keep.tile([P, 2 * R + N], U8, name="weight_rows", align_bytes=64)
+        staged = keep.tile([P, SCALE_ROW], U8, name="staged", align_bytes=64)
+        planes = keep.tile([P, 2, SCALE_ROW], U8, name="planes", align_bytes=64)
+        nc.vector.memset(weight_rows[:, 2 * R :].bitcast(I32), 0)
+        nc.sync.dma_start(table_rows[0:32].bitcast(I32), tab_scales.rearrange("a b t -> b a t").bitcast(I32))
+        nc.sync.dma_start(weight_rows[0:32, 0:R].bitcast(I32), wg_scales.rearrange("a b n -> b a n").bitcast(I32))
+        nc.sync.dma_start(weight_rows[0:32, R : 2 * R].bitcast(I32), wu_scales.rearrange("a b n -> b a n").bitcast(I32))
+        nc.sync.dma_start(weight_rows[0:32:2, 2 * R :].bitcast(I32), wd_scales[0].bitcast(I32))
         for rows in (slice(32, 64), slice(64, 128)):
-            nc.gpsimd.memset(wsc[rows, 0 : 2 * R].bitcast(I32), 0)
-            nc.vector.memset(tsc[rows].bitcast(I32), 0)
-        nc.gpsimd.memset(both[:].bitcast(I32), 0)
+            nc.gpsimd.memset(weight_rows[rows, 0 : 2 * R].bitcast(I32), 0)
+            nc.vector.memset(table_rows[rows].bitcast(I32), 0)
+        nc.gpsimd.memset(planes[:].bitcast(I32), 0)
 
-        wg = shared.tile([P, 70 * KB], U8, name="wg", align_bytes=64, offset=0)
-        tabw = keep.tile([P, T], I32, name="tabw", align_bytes=64)
-        nc.sync.dma_start(wg[:, 0 : 4 * R].bitcast(I32).rearrange("p (a n) -> p a n", a=2),
+        landing = shared.tile([P, LANDING_BYTES], U8, name="landing", align_bytes=64, offset=0)
+        wg = landing[:, 0 : 4 * R]
+        table = keep.tile([P, T], I32, name="table", align_bytes=64)
+        nc.sync.dma_start(wg.bitcast(I32).rearrange("p (a n) -> p a n", a=2),
                           wg_words.rearrange("a p n -> p a n").bitcast(I32))
-        nc.sync.dma_start(tabw[:], tab_words[0].rearrange("p t b -> p (t b)").bitcast(I32))
+        nc.sync.dma_start(table[:], tab_words[0].rearrange("p t b -> p (t b)").bitcast(I32))
         wu = keep.tile([P, 2 * R], I32, name="wu", align_bytes=64)
         nc.sync.dma_start(wu[:].rearrange("p (a n) -> p a n", a=2), wu_words.rearrange("a p n i -> p a (n i)").bitcast(I32))
 
-        nc.gpsimd.tensor_copy(staged[:, J:].rearrange("p (w t c i) -> p w c t i", w=3, t=4, i=16),
-                              wsc[:].rearrange("p (w c i t) -> p w c t i", w=3, t=4, i=16))
-        picked_sc = shared.tile([P, J], U8, name="picked_sc", align_bytes=64, offset=70 * KB)
-        nc.vector.tensor_copy(picked_sc[:], tsc[:].indirect(offsets[:]))
-        nc.vector.tensor_copy(staged[0:32, 0:J].bitcast(I32), picked_sc[0:32].bitcast(I32))
+        nc.gpsimd.tensor_copy(staged[:, WG_SCALES:].rearrange("p (w t c i) -> p w c t i", w=3, t=4, i=16),
+                              weight_rows[:].rearrange("p (w c i t) -> p w c t i", w=3, t=4, i=16))
+        picked_rows = shared.tile([P, J], U8, name="picked_rows", align_bytes=64, offset=LANDING_BYTES)
+        nc.vector.tensor_copy(picked_rows[:], table_rows[:].indirect(offsets[:]))
+        nc.vector.tensor_copy(staged[0:32, 0:J].bitcast(I32), picked_rows[0:32].bitcast(I32))
         for q in (0, 2, 1, 3):
-            nc.sync.dma_start(both[32 * q : 32 * q + 4].bitcast(I32), staged[8 * q : 8 * q + 8].bitcast(I32))
+            nc.sync.dma_start(planes[32 * q : 32 * q + 4].bitcast(I32), staged[8 * q : 8 * q + 8].bitcast(I32))
 
-        wg_dealt = shared.tile([P, 4 * R], U8, name="wg_dealt", align_bytes=64, offset=70 * KB)
+        wg_dealt = shared.tile([P, 4 * R], U8, name="wg_dealt", align_bytes=64, offset=LANDING_BYTES)
         nc.vector.tensor_copy(wg_dealt[:].bitcast(U16).rearrange("p (a t c i) -> p a c t i", a=2, t=4, i=8),
-                              wg[:, 0 : 4 * R].bitcast(U16).rearrange("p (a c i t) -> p a c t i", a=2, t=4, i=8))
+                              wg.bitcast(U16).rearrange("p (a c i t) -> p a c t i", a=2, t=4, i=8))
 
         warm = psum.tile([P, R], F32, name="warm", tag="y", bufs=3)
-        for w in range(4):
-            early = wg_dealt[:, 0 : 2 * P].bitcast(FP4X4) if w < 2 else wu[:, 0:P].bitcast(FP8X4)
-            nc.tensor.matmul_mx(out=warm[:], lhsT=early, lhsT_scale=wsc[:, 0:P],
-                                rhs=wg_dealt[:, 0 : 2 * R].bitcast(FP4X4), rhs_scale=wsc[:, 0:R], start=True, stop=True)
-        wd = shared.tile([P, N], I32, name="wd", align_bytes=64, offset=4 * KB)
+        for stationary in 2 * [wg_dealt[:, 0 : 2 * P].bitcast(FP4X4)] + 2 * [wu[:, 0:P].bitcast(FP8X4)]:
+            nc.tensor.matmul_mx(out=warm[:], lhsT=stationary, lhsT_scale=weight_rows[:, 0:P],
+                                rhs=wg_dealt[:, 0 : 2 * R].bitcast(FP4X4), rhs_scale=weight_rows[:, 0:R],
+                                start=True, stop=True)
+
+        wd = shared.tile([P, N], I32, name="wd", align_bytes=64, offset=WD_AT)
         nc.sync.dma_start(wd[:], wd_words[0].rearrange("p n i -> p (n i)").bitcast(I32))
-        r_rows = rT.rearrange("(p t) c -> p t c", t=4)
-        res = []
+        r_slices = rT.rearrange("(p t) c -> p t c", t=4)
+        windows = []
         for t in range(4):
-            window = shared.tile([P, T], F32, name=f"res{t}", align_bytes=64, offset=(6 + 16 * t) * KB)
-            nc.sync.dma_start(window[:], r_rows[:, t, :])
-            res.append(window)
+            window = shared.tile([P, T], F32, name=f"window{t}", align_bytes=64, offset=WINDOWS_AT + t * 4 * T)
+            nc.sync.dma_start(window[:], r_slices[:, t, :])
+            windows.append(window)
 
         parted = []
 
-        def pick_words(hf):
-            picked = shared.tile([P, HALF], U32, name=f"picked{hf}", align_bytes=64, offset=(96 + hf) * KB)
-            nc.vector.tensor_copy(picked[:], tabw[:].bitcast(U32).indirect(cols(hf * HALF, HALF)))
+        def pick_words(hf, pieces):
+            picked = shared.tile([P, HALF], U32, name=f"picked{hf}", align_bytes=64, offset=PICKED_AT + hf * KB)
+            nc.vector.tensor_copy(picked[:], table[:].bitcast(U32).indirect(listed(hf * HALF, HALF)))
             words = keep.tile([P, 4 * HALF], U8, name=f"parted{hf}", align_bytes=64)
-            nc.vector.tensor_copy(
-                words[:].bitcast(U16).rearrange("p (d c i) -> p c d i", d=2, i=8),
-                picked[:].bitcast(U16).rearrange("p (c i d) -> p c d i", d=2, i=8),
-            )
+            lines = HALF // 8 // pieces
+            for first in range(0, HALF // 8, lines):
+                nc.vector.tensor_copy(
+                    words[:].bitcast(U16).rearrange("p (a c i) -> p c a i", a=2, i=8)[:, first : first + lines],
+                    picked[:].bitcast(U16).rearrange("p (c i a) -> p c a i", a=2, i=8)[:, first : first + lines],
+                )
             parted.append(words)
 
-        pick_words(0)
-        wu_dealt = shared.tile([P, 2 * R], I32, name="wu_dealt", align_bytes=64, offset=93 * KB)
+        pick_words(0, 2)
+        wu_dealt = shared.tile([P, 2 * R], I32, name="wu_dealt", align_bytes=64, offset=WU_DEALT_AT)
         nc.vector.tensor_copy(wu_dealt[:].rearrange("p (a t c i) -> p a c t i", a=2, t=4, i=4),
                               wu[:].rearrange("p (a c i t) -> p a c t i", a=2, t=4, i=4))
-        pick_words(1)
+        pick_words(1, 1)
         wd_dealt = keep.tile([P, N], I32, name="wd_dealt", align_bytes=64)
         nc.vector.tensor_copy(wd_dealt[:].rearrange("p (t c i) -> p c t i", t=4, i=4),
                               wd[:].rearrange("p (c i t) -> p c t i", t=4, i=4))
 
-        sums0 = keep.tile([P, 4, HALF], F32, name="sums0", align_bytes=64)
-        sums1 = keep.tile([P, 5 * HALF], F32, name="sums1", align_bytes=64)
-        sums = [sums0[:], sums1[:, 0 : 4 * HALF].rearrange("p (t j) -> p t j", t=4)]
-        planes = (plane0, plane1)
+        first_half = keep.tile([P, 4, HALF], F32, name="first_half", align_bytes=64)
+        second_half = keep.tile([P, 4 * HALF + 2 * QUARTER], F32, name="second_half", align_bytes=64)
+        sums = [first_half[:], second_half[:, 0 : 4 * HALF].rearrange("p (t j) -> p t j", t=4)]
+        quarter_rows = second_half[:].rearrange("p (e x) -> p e x", x=QUARTER)
+
+        def table_operand(a, first, count):
+            hf, j0 = divmod(first, HALF)
+            b0 = 2 * (a * HALF + j0)
+            return dict(rhs=parted[hf][:, b0 : b0 + 2 * count].bitcast(FP4X4), rhs_scale=planes[:, a, first : first + count])
 
         def gates(c, gate):
-            hf, j0 = divmod(c * QUARTER, HALF)
             for u in range(2):
                 ga = psum.tile([P, 2, QUARTER], F32, name="ga", bufs=3)
                 for e in range(2):
                     t = 2 * u + e
                     for a in range(2):
                         c0 = a * R + t * P
-                        b0 = 2 * (a * HALF + j0)
                         nc.tensor.matmul_mx(
                             out=ga[:, e, :], lhsT=wg_dealt[:, 2 * c0 : 2 * (c0 + P)].bitcast(FP4X4),
-                            lhsT_scale=planes[a][:, J + t * P : J + (t + 1) * P],
-                            rhs=parted[hf][:, b0 : b0 + 2 * QUARTER].bitcast(FP4X4),
-                            rhs_scale=planes[a][:, c * QUARTER : (c + 1) * QUARTER], start=(a == 0), stop=(a == 1))
+                            lhsT_scale=planes[:, a, WG_SCALES + t * P : WG_SCALES + (t + 1) * P],
+                            start=(a == 0), stop=(a == 1), **table_operand(a, c * QUARTER, QUARTER))
                 nc.scalar.activation(gate[:, u, :].rearrange("p (j e) -> p j e", e=2), ga[:].rearrange("p e j -> p j e"), SIGMOID)
 
-        def gated(jt, gate, h_out):
-            hf, j0 = divmod(jt * P, HALF)
+        def gated(c, s, gate, h):
             ub = psum.tile([P, 4, P], F32, name="ub", bufs=2)
             for t in range(4):
                 for a in range(2):
                     c0 = a * R + t * P
-                    s0 = J + R + t * P
-                    b0 = 2 * (a * HALF + j0)
                     nc.tensor.matmul_mx(
-                        out=ub[:, t, :], lhsT=wu_dealt[:, c0 : c0 + P].bitcast(FP8X4), lhsT_scale=planes[a][:, s0 : s0 + P],
-                        rhs=parted[hf][:, b0 : b0 + 2 * P].bitcast(FP4X4),
-                        rhs_scale=planes[a][:, jt * P : (jt + 1) * P], start=(a == 0), stop=(a == 1))
-            s = jt % 2
-            nc.vector.tensor_tensor(h_out.rearrange("p (j u e) -> p j u e", u=2, e=2),
+                        out=ub[:, t, :], lhsT=wu_dealt[:, c0 : c0 + P].bitcast(FP8X4),
+                        lhsT_scale=planes[:, a, WU_SCALES + t * P : WU_SCALES + (t + 1) * P],
+                        start=(a == 0), stop=(a == 1), **table_operand(a, c * QUARTER + s * P, P))
+            nc.vector.tensor_tensor(h[:, 4 * s * P : 4 * (s + 1) * P].rearrange("p (j u e) -> p j u e", u=2, e=2),
                                     ub[:].rearrange("p (u e) j -> p j u e", u=2),
                                     gate[:, :, 2 * s * P : 2 * (s + 1) * P].rearrange("p u (j e) -> p j u e", e=2), MULT)
 
-        y_rows = {}
-
-        def quantise_h(h_woven):
+        def quantise(h):
             h_codes = ring.tile([P, QUARTER], I32, name="h_codes", align_bytes=64)
             h_scales = ring.tile([P, QUARTER], U8, name="h_scales", align_bytes=64)
-            nc.vector.quantize_mx(out=h_codes[:].bitcast(FP8X4), scales=h_scales[:], in_=h_woven)
+            nc.vector.quantize_mx(out=h_codes[:].bitcast(FP8X4), scales=h_scales[:], in_=h[:])
             return h_codes, h_scales
 
-        def second_stage(h_codes, h_scales, c, pairs):
-            for u in pairs:
+        y_pairs = {(1, 1): quarter_rows[:, 3:9:5, :], (2, 1): quarter_rows[:, 1:10:8, :]}
+
+        def second_stage(c, h_codes, h_scales):
+            for u in range(2):
                 y = psum.tile([P, 2, QUARTER], F32, name="y", bufs=3)
                 for e in range(2):
                     t = 2 * u + e
-                    s0 = J + 2 * R + t * P
                     nc.tensor.matmul_mx(out=y[:, e, :], lhsT=wd_dealt[:, t * P : (t + 1) * P].bitcast(FP8X4),
-                                        lhsT_scale=plane0[:, s0 : s0 + P],
+                                        lhsT_scale=planes[:, 0, WD_SCALES + t * P : WD_SCALES + (t + 1) * P],
                                         rhs=h_codes[:].bitcast(FP8X4), rhs_scale=h_scales[:], start=True, stop=True)
-                if (c, u) == (1, 1):
-                    rows = sums1[:, 768:2304].rearrange("p (e x) -> p e x", x=QUARTER)[:, 0:6:5, :]
-                elif (c, u) == (2, 1):
-                    rows = sums1[:, 256:2560].rearrange("p (e x) -> p e x", x=QUARTER)[:, 0:9:8, :]
-                else:
-                    rows = keep.tile([P, 2, QUARTER], F32, name=f"y_rows{c}{u}", align_bytes=64)[:]
-                nc.scalar.copy(rows, y[:])
-                y_rows[c, u] = rows
+                if (c, u) not in y_pairs:
+                    y_pairs[c, u] = keep.tile([P, 2, QUARTER], F32, name=f"y_pair{c}{u}", align_bytes=64)[:]
+                nc.scalar.copy(y_pairs[c, u], y[:])
 
-        out_rows = out_0.rearrange("(p t) j -> p t j", t=4)
-        woven = [keep.tile([P, QUARTER, 4], BF16, name=f"woven{c}", align_bytes=64)[:] for c in range(4)]
+        out_slices = out_0.rearrange("(p t) j -> p t j", t=4)
+        rounded = [keep.tile([P, QUARTER, 4], BF16, name=f"rounded{c}", align_bytes=64) for c in range(4)]
 
-        def add_residual(dst, t, c):
-            nc.vector.tensor_tensor(dst, res[t][:].indirect(cols(c * QUARTER, QUARTER)), y_rows[c, t // 2][:, t % 2, :], ADD)
-
-        def cell(t, c):
+        def add_residual(t, c):
             hf, j0 = divmod(c * QUARTER, HALF)
-            add_residual(sums[hf][:, t, j0 : j0 + QUARTER], t, c)
+            nc.vector.tensor_tensor(sums[hf][:, t, j0 : j0 + QUARTER], windows[t][:].indirect(listed(c * QUARTER, QUARTER)),
+                                    y_pairs[c, t // 2][:, t % 2, :], ADD)
             if t == 3:
-                weave = nc.scalar.copy if c < 3 else nc.vector.tensor_copy
-                weave(woven[c].rearrange("p (c i) t -> p c t i", i=2),
-                      sums[hf][:, :, j0 : j0 + QUARTER].rearrange("p t (c i) -> p c t i", i=2))
-            if c % 2 == 1 and t > 0:
-                rows = slice(0, 2) if t == 1 else slice(t, t + 1)
-                nc.sync.dma_start(out_rows[:, rows, hf * HALF : (hf + 1) * HALF], sums[hf][:, rows, :])
+                round_copy = nc.vector.tensor_copy if c == LAST else nc.scalar.copy
+                round_copy(rounded[c][:].rearrange("p (c i) t -> p c t i", i=2),
+                           sums[hf][:, :, j0 : j0 + QUARTER].rearrange("p t (c i) -> p c t i", i=2))
+            if c % 2 == 1 and t >= 2:
+                done = slice(0, 3) if t == 2 else slice(3, 4)
+                nc.sync.dma_start(out_slices[:, done, hf * HALF : (hf + 1) * HALF], sums[hf][:, done, :])
 
         for c in range(4):
-            h_woven = ring.tile([P, 4 * QUARTER], BF16, name="h_woven", align_bytes=64)[:]
-            gate = ring.tile([P, 2, HALF], F32, name="gate", align_bytes=64)[:]
+            h = ring.tile([P, 4 * QUARTER], BF16, name="h", align_bytes=64)
+            gate = ring.tile([P, 2, 2 * QUARTER], F32, name="gate", align_bytes=64)
             gates(c, gate)
             for s in range(2):
-                gated(2 * c + s, gate, h_woven[:, s * HALF : (s + 1) * HALF])
+                gated(c, s, gate, h)
             if c > 0:
-                second_stage(*quantised, c - 1, (0, 1))
-            quantised = quantise_h(h_woven)
-        second_stage(*quantised, 3, (0, 1))
-        for t, c in ((0, 0), (1, 0), (0, 1), (1, 1), (0, 2), (1, 2), (2, 0), (2, 1), (2, 2), (0, 3), (1, 3), (2, 3)):
-            cell(t, c)
+                second_stage(c - 1, *quantised)
+            quantised = quantise(h)
+        second_stage(LAST, *quantised)
+
+        for c in range(LAST):
+            for t in range(2):
+                add_residual(t, c)
+        for c in range(LAST):
+            add_residual(2, c)
+        for t in range(3):
+            add_residual(t, LAST)
         for c in range(4):
-            cell(3, c)
-        o_codes = keep.tile([P, J], I32, name="o_codes", align_bytes=64)
-        o_scales = keep.tile([P, J], U8, name="o_scales", align_bytes=64)
+            add_residual(3, c)
+
+        out_codes = keep.tile([P, J], I32, name="out_codes", align_bytes=64)
+        out_scales = keep.tile([P, J], U8, name="out_scales", align_bytes=64)
         code_rows = out_1[0].rearrange("p j b -> p (j b)").bitcast(I32)
         for c in range(4):
             span = slice(c * QUARTER, (c + 1) * QUARTER)
-            nc.vector.quantize_mx(out=o_codes[:, span].bitcast(FP8X4), scales=o_scales[:, span],
-                                  in_=woven[c].rearrange("p j t -> p (j t)"))
-            if c > 0:
-                done = slice(0, HALF) if c == 1 else span
-                nc.sync.dma_start(code_rows[:, done], o_codes[:, done])
+            nc.vector.quantize_mx(out=out_codes[:, span].bitcast(FP8X4), scales=out_scales[:, span],
+                                  in_=rounded[c][:].rearrange("p j t -> p (j t)"))
+            if c % 2 == 1:
+                half = slice((c // 2) * HALF, (c // 2 + 1) * HALF)
+                nc.sync.dma_start(code_rows[:, half], out_codes[:, half])
         for q in range(4):
             queue = nc.sync if q % 2 == 0 else nc.scalar
-            queue.dma_start(out_2[0, 4 * q : 4 * q + 4, :].bitcast(I32), o_scales[32 * q : 32 * q + 4].bitcast(I32))
+            queue.dma_start(out_2[0, 4 * q : 4 * q + 4, :].bitcast(I32), out_scales[32 * q : 32 * q + 4].bitcast(I32))

@@ -21,6 +21,7 @@ P = 128
 HALF = 512
 QUARTER = 256
 LAST = J // QUARTER - 1
+ROUNDED_ON_SCALAR = 640
 KB = 1024
 
 WG_SCALES, WU_SCALES, WD_SCALES, SCALE_ROW = J, J + R, J + 2 * R, J + 2 * R + N
@@ -186,11 +187,13 @@ def tile_list_gmlpt_sigm_resLP_kernel(
             nc.vector.tensor_tensor(sums[hf][:, t, j0 : j0 + QUARTER], windows[t][:].indirect(listed(c * QUARTER, QUARTER)),
                                     y_pairs[c, t // 2][:, t % 2, :], ADD)
             if t == 3:
-                round_copy = nc.vector.tensor_copy if c == LAST else nc.scalar.copy
-                round_copy(rounded[c][:].rearrange("p (c i) t -> p c t i", i=2),
-                           sums[hf][:, :, j0 : j0 + QUARTER].rearrange("p t (c i) -> p c t i", i=2))
-            if c % 2 == 1 and t >= 2:
-                done = slice(0, 3) if t == 2 else slice(3, 4)
+                on_scalar = min(QUARTER, max(0, ROUNDED_ON_SCALAR - c * QUARTER))
+                for round_copy, first, end in ((nc.scalar.copy, 0, on_scalar), (nc.vector.tensor_copy, on_scalar, QUARTER)):
+                    if end > first:
+                        round_copy(rounded[c][:, first:end, :].rearrange("p (c i) t -> p c t i", i=4),
+                                   sums[hf][:, :, j0 + first : j0 + end].rearrange("p t (c i) -> p c t i", i=4))
+            if c % 2 == 1 and t >= 1:
+                done = slice(0, 2) if t == 1 else slice(t, t + 1)
                 nc.sync.dma_start(out_slices[:, done, hf * HALF : (hf + 1) * HALF], sums[hf][:, done, :])
 
         for c in range(4):
@@ -221,9 +224,9 @@ def tile_list_gmlpt_sigm_resLP_kernel(
             span = slice(c * QUARTER, (c + 1) * QUARTER)
             nc.vector.quantize_mx(out=out_codes[:, span].bitcast(FP8X4), scales=out_scales[:, span],
                                   in_=rounded[c][:].rearrange("p j t -> p (j t)"))
-            if c % 2 == 1:
-                half = slice((c // 2) * HALF, (c // 2 + 1) * HALF)
-                nc.sync.dma_start(code_rows[:, half], out_codes[:, half])
+            if c > 0:
+                done = slice(0, HALF) if c == 1 else span
+                nc.sync.dma_start(code_rows[:, done], out_codes[:, done])
         for q in range(4):
             queue = nc.sync if q % 2 == 0 else nc.scalar
             queue.dma_start(out_2[0, 4 * q : 4 * q + 4, :].bitcast(I32), out_scales[32 * q : 32 * q + 4].bitcast(I32))

@@ -21,14 +21,15 @@ P = 128
 HALF = 512
 QUARTER = 256
 LAST = J // QUARTER - 1
-ROUNDED_ON_SCALAR = 640
 KB = 1024
 
 WG_SCALES, WU_SCALES, WD_SCALES, SCALE_ROW = J, J + R, J + 2 * R, J + 2 * R + N
 
-WD_AT = 4 * KB
-WINDOWS_AT = 6 * KB
+WU_AT = 2 * KB
+WD_AT = 6 * KB
+WINDOWS_AT = 8 * KB
 LANDING_BYTES = WINDOWS_AT + 4 * 4 * T
+ROUNDED_AT = LANDING_BYTES + 3 * KB
 WU_DEALT_AT = 93 * KB
 PICKED_AT = WU_DEALT_AT + 3 * KB
 
@@ -51,7 +52,7 @@ def tile_list_gmlpt_sigm_resLP_kernel(
             return offsets[:, first // 16 : (first + count) // 16]
 
         table_rows = keep.tile([P, T], U8, name="table_rows", align_bytes=64)
-        weight_rows = keep.tile([P, 2 * R + N], U8, name="weight_rows", align_bytes=64)
+        weight_rows = shared.tile([P, 2 * R + N], U8, name="weight_rows", align_bytes=64, offset=LANDING_BYTES)
         staged = keep.tile([P, SCALE_ROW], U8, name="staged", align_bytes=64)
         planes = keep.tile([P, 2, SCALE_ROW], U8, name="planes", align_bytes=64)
         nc.vector.memset(weight_rows[:, 2 * R :].bitcast(I32), 0)
@@ -59,36 +60,39 @@ def tile_list_gmlpt_sigm_resLP_kernel(
         nc.sync.dma_start(weight_rows[0:32, 0:R].bitcast(I32), wg_scales.rearrange("a b n -> b a n").bitcast(I32))
         nc.sync.dma_start(weight_rows[0:32, R : 2 * R].bitcast(I32), wu_scales.rearrange("a b n -> b a n").bitcast(I32))
         nc.sync.dma_start(weight_rows[0:32:2, 2 * R :].bitcast(I32), wd_scales[0].bitcast(I32))
-        for rows in (slice(32, 64), slice(64, 128)):
-            nc.gpsimd.memset(weight_rows[rows, 0 : 2 * R].bitcast(I32), 0)
-            nc.vector.memset(table_rows[rows].bitcast(I32), 0)
+        nc.vector.memset(table_rows[32:64].bitcast(I32), 0)
+        nc.gpsimd.memset(table_rows[64:128].bitcast(I32), 0)
         nc.gpsimd.memset(planes[:].bitcast(I32), 0)
+        for rows in (slice(32, 64), slice(64, 128)):
+            nc.vector.memset(weight_rows[rows, 0 : 2 * R].bitcast(I32), 0)
 
         landing = shared.tile([P, LANDING_BYTES], U8, name="landing", align_bytes=64, offset=0)
-        wg = landing[:, 0 : 4 * R]
+        wg = [landing[:, 0 : 2 * R], keep.tile([P, 2 * R], U8, name="wg_second", align_bytes=64)[:]]
         table = keep.tile([P, T], I32, name="table", align_bytes=64)
-        nc.sync.dma_start(wg.bitcast(I32).rearrange("p (a n) -> p a n", a=2),
-                          wg_words.rearrange("a p n -> p a n").bitcast(I32))
+        nc.sync.dma_start(wg[0].bitcast(I32), wg_words[0].bitcast(I32))
         nc.sync.dma_start(table[:], tab_words[0].rearrange("p t b -> p (t b)").bitcast(I32))
-        wu = keep.tile([P, 2 * R], I32, name="wu", align_bytes=64)
-        nc.sync.dma_start(wu[:].rearrange("p (a n) -> p a n", a=2), wu_words.rearrange("a p n i -> p a (n i)").bitcast(I32))
+        nc.sync.dma_start(wg[1].bitcast(I32), wg_words[1].bitcast(I32))
 
         nc.gpsimd.tensor_copy(staged[:, WG_SCALES:].rearrange("p (w t c i) -> p w c t i", w=3, t=4, i=16),
                               weight_rows[:].rearrange("p (w c i t) -> p w c t i", w=3, t=4, i=16))
-        picked_rows = shared.tile([P, J], U8, name="picked_rows", align_bytes=64, offset=LANDING_BYTES)
+        picked_rows = keep.tile([P, J], U8, name="picked_rows", align_bytes=64)
         nc.vector.tensor_copy(picked_rows[:], table_rows[:].indirect(offsets[:]))
         nc.vector.tensor_copy(staged[0:32, 0:J].bitcast(I32), picked_rows[0:32].bitcast(I32))
         for q in (0, 2, 1, 3):
             nc.sync.dma_start(planes[32 * q : 32 * q + 4].bitcast(I32), staged[8 * q : 8 * q + 8].bitcast(I32))
 
         wg_dealt = shared.tile([P, 4 * R], U8, name="wg_dealt", align_bytes=64, offset=LANDING_BYTES)
-        nc.vector.tensor_copy(wg_dealt[:].bitcast(U16).rearrange("p (a t c i) -> p a c t i", a=2, t=4, i=8),
-                              wg.bitcast(U16).rearrange("p (a c i t) -> p a c t i", a=2, t=4, i=8))
+        for a in range(2):
+            nc.vector.tensor_copy(wg_dealt[:, 2 * a * R : 2 * (a + 1) * R].bitcast(U16).rearrange("p (t c i) -> p c t i", t=4, i=8),
+                                  wg[a].bitcast(U16).rearrange("p (c i t) -> p c t i", t=4, i=8))
+
+        wu = shared.tile([P, 2 * R], I32, name="wu", align_bytes=64, offset=WU_AT)
+        nc.sync.dma_start(wu[:].rearrange("p (a n) -> p a n", a=2), wu_words.rearrange("a p n i -> p a (n i)").bitcast(I32))
 
         warm = psum.tile([P, R], F32, name="warm", tag="y", bufs=3)
-        for stationary in 2 * [wg_dealt[:, 0 : 2 * P].bitcast(FP4X4)] + 2 * [wu[:, 0:P].bitcast(FP8X4)]:
-            nc.tensor.matmul_mx(out=warm[:], lhsT=stationary, lhsT_scale=weight_rows[:, 0:P],
-                                rhs=wg_dealt[:, 0 : 2 * R].bitcast(FP4X4), rhs_scale=weight_rows[:, 0:R],
+        for stationary in 4 * [wg_dealt[:, 0 : 2 * P].bitcast(FP4X4)]:
+            nc.tensor.matmul_mx(out=warm[:], lhsT=stationary, lhsT_scale=staged[:, WG_SCALES : WG_SCALES + P],
+                                rhs=wg_dealt[:, 0 : 2 * R].bitcast(FP4X4), rhs_scale=staged[:, WG_SCALES : WG_SCALES + R],
                                 start=True, stop=True)
 
         wd = shared.tile([P, N], I32, name="wd", align_bytes=64, offset=WD_AT)
@@ -103,7 +107,7 @@ def tile_list_gmlpt_sigm_resLP_kernel(
         parted = []
 
         def pick_words(hf, pieces):
-            picked = shared.tile([P, HALF], U32, name=f"picked{hf}", align_bytes=64, offset=PICKED_AT + hf * KB)
+            picked = shared.tile([P, HALF], U32, name=f"picked{hf}", align_bytes=64, offset=(PICKED_AT, WU_AT)[hf])
             nc.vector.tensor_copy(picked[:], table[:].bitcast(U32).indirect(listed(hf * HALF, HALF)))
             words = keep.tile([P, 4 * HALF], U8, name=f"parted{hf}", align_bytes=64)
             lines = HALF // 8 // pieces
@@ -159,10 +163,13 @@ def tile_list_gmlpt_sigm_resLP_kernel(
                                     ub[:].rearrange("p (u e) j -> p j u e", u=2),
                                     gate[:, :, 2 * s * P : 2 * (s + 1) * P].rearrange("p u (j e) -> p j u e", e=2), MULT)
 
-        def quantise(h):
-            h_codes = ring.tile([P, QUARTER], I32, name="h_codes", align_bytes=64)
+        def quantise(c, h):
+            if c == LAST:
+                h_codes = shared.tile([P, 4 * QUARTER], I32, name="h_codes_wide", align_bytes=64, offset=ROUNDED_AT)[:, 0:QUARTER]
+            else:
+                h_codes = ring.tile([P, QUARTER], I32, name="h_codes", align_bytes=64)[:]
             h_scales = ring.tile([P, QUARTER], U8, name="h_scales", align_bytes=64)
-            nc.vector.quantize_mx(out=h_codes[:].bitcast(FP8X4), scales=h_scales[:], in_=h[:])
+            nc.vector.quantize_mx(out=h_codes.bitcast(FP8X4), scales=h_scales[:], in_=h[:])
             return h_codes, h_scales
 
         y_pairs = {(1, 1): quarter_rows[:, 3:9:5, :], (2, 1): quarter_rows[:, 1:10:8, :]}
@@ -174,24 +181,28 @@ def tile_list_gmlpt_sigm_resLP_kernel(
                     t = 2 * u + e
                     nc.tensor.matmul_mx(out=y[:, e, :], lhsT=wd_dealt[:, t * P : (t + 1) * P].bitcast(FP8X4),
                                         lhsT_scale=planes[:, 0, WD_SCALES + t * P : WD_SCALES + (t + 1) * P],
-                                        rhs=h_codes[:].bitcast(FP8X4), rhs_scale=h_scales[:], start=True, stop=True)
+                                        rhs=h_codes.bitcast(FP8X4), rhs_scale=h_scales[:], start=True, stop=True)
                 if (c, u) not in y_pairs:
                     y_pairs[c, u] = keep.tile([P, 2, QUARTER], F32, name=f"y_pair{c}{u}", align_bytes=64)[:]
                 nc.scalar.copy(y_pairs[c, u], y[:])
 
         out_slices = out_0.rearrange("(p t) j -> p t j", t=4)
-        rounded = [keep.tile([P, QUARTER, 4], BF16, name=f"rounded{c}", align_bytes=64) for c in range(4)]
+        rounded = [shared.tile([P, QUARTER, 4], BF16, name=f"rounded{c}", align_bytes=64, offset=ROUNDED_AT + 2 * c * KB)
+                   for c in range(4)]
+
+        def round_pair(u, c):
+            hf, j0 = divmod(c * QUARTER, HALF)
+            nc.scalar.copy(rounded[c][:, :, 2 * u : 2 * u + 2],
+                           sums[hf][:, 2 * u : 2 * u + 2, j0 : j0 + QUARTER].rearrange("p e j -> p j e"))
 
         def add_residual(t, c):
             hf, j0 = divmod(c * QUARTER, HALF)
-            nc.vector.tensor_tensor(sums[hf][:, t, j0 : j0 + QUARTER], windows[t][:].indirect(listed(c * QUARTER, QUARTER)),
-                                    y_pairs[c, t // 2][:, t % 2, :], ADD)
-            if t == 3:
-                on_scalar = min(QUARTER, max(0, ROUNDED_ON_SCALAR - c * QUARTER))
-                for round_copy, first, end in ((nc.scalar.copy, 0, on_scalar), (nc.vector.tensor_copy, on_scalar, QUARTER)):
-                    if end > first:
-                        round_copy(rounded[c][:, first:end, :].rearrange("p (c i) t -> p c t i", i=4),
-                                   sums[hf][:, :, j0 + first : j0 + end].rearrange("p t (c i) -> p c t i", i=4))
+            picked = early[:, j0 : j0 + QUARTER] if (t, hf) == (0, 1) else windows[t][:].indirect(listed(c * QUARTER, QUARTER))
+            nc.vector.tensor_tensor(sums[hf][:, t, j0 : j0 + QUARTER], picked, y_pairs[c, t // 2][:, t % 2, :], ADD)
+            if (t, c) == (1, 1):
+                round_pair(0, 0)
+            if t == 3 or (t == 1 and c > 0):
+                round_pair(t // 2, c)
             if c % 2 == 1 and t >= 1:
                 done = slice(0, 2) if t == 1 else slice(t, t + 1)
                 nc.sync.dma_start(out_slices[:, done, hf * HALF : (hf + 1) * HALF], sums[hf][:, done, :])
@@ -204,9 +215,11 @@ def tile_list_gmlpt_sigm_resLP_kernel(
                 gated(c, s, gate, h)
             if c > 0:
                 second_stage(c - 1, *quantised)
-            quantised = quantise(h)
+            quantised = quantise(c, h)
         second_stage(LAST, *quantised)
 
+        early = keep.tile([P, HALF], F32, name="early", align_bytes=64)
+        nc.vector.tensor_copy(early[:], windows[0][:].indirect(listed(HALF, HALF)))
         for c in range(LAST):
             for t in range(2):
                 add_residual(t, c)

@@ -57,9 +57,9 @@ def tile_list_gmlpt_sigm_resLP_kernel(
         planes = keep.tile([P, 2, SCALE_ROW], U8, name="planes", align_bytes=64)
         nc.vector.memset(weight_rows[:, 2 * R :].bitcast(I32), 0)
         nc.sync.dma_start(table_rows[0:32].bitcast(I32), tab_scales.rearrange("a b t -> b a t").bitcast(I32))
-        nc.sync.dma_start(weight_rows[0:32, 0:R].bitcast(I32), wg_scales.rearrange("a b n -> b a n").bitcast(I32))
-        nc.sync.dma_start(weight_rows[0:32, R : 2 * R].bitcast(I32), wu_scales.rearrange("a b n -> b a n").bitcast(I32))
-        nc.sync.dma_start(weight_rows[0:32:2, 2 * R :].bitcast(I32), wd_scales[0].bitcast(I32))
+        nc.scalar.dma_start(weight_rows[0:32, 0:R].bitcast(I32), wg_scales.rearrange("a b n -> b a n").bitcast(I32))
+        nc.scalar.dma_start(weight_rows[0:32, R : 2 * R].bitcast(I32), wu_scales.rearrange("a b n -> b a n").bitcast(I32))
+        nc.scalar.dma_start(weight_rows[0:32:2, 2 * R :].bitcast(I32), wd_scales[0].bitcast(I32))
         nc.vector.memset(table_rows[32:64].bitcast(I32), 0)
         nc.gpsimd.memset(table_rows[64:128].bitcast(I32), 0)
         nc.gpsimd.memset(planes[:].bitcast(I32), 0)
@@ -190,21 +190,29 @@ def tile_list_gmlpt_sigm_resLP_kernel(
         rounded = [shared.tile([P, QUARTER, 4], BF16, name=f"rounded{c}", align_bytes=64, offset=ROUNDED_AT + 2 * c * KB)
                    for c in range(4)]
 
-        def round_pair(u, c):
-            hf, j0 = divmod(c * QUARTER, HALF)
-            nc.scalar.copy(rounded[c][:, :, 2 * u : 2 * u + 2],
-                           sums[hf][:, 2 * u : 2 * u + 2, j0 : j0 + QUARTER].rearrange("p e j -> p j e"))
+        def round_pair(u, c, first=0, count=QUARTER):
+            hf, j0 = divmod(c * QUARTER + first, HALF)
+            nc.scalar.copy(rounded[c][:, first : first + count, 2 * u : 2 * u + 2],
+                           sums[hf][:, 2 * u : 2 * u + 2, j0 : j0 + count].rearrange("p e j -> p j e"))
 
         def add_residual(t, c):
             hf, j0 = divmod(c * QUARTER, HALF)
-            picked = early[:, j0 : j0 + QUARTER] if (t, hf) == (0, 1) else windows[t][:].indirect(listed(c * QUARTER, QUARTER))
-            nc.vector.tensor_tensor(sums[hf][:, t, j0 : j0 + QUARTER], picked, y_pairs[c, t // 2][:, t % 2, :], ADD)
+            count = P if (t, c) == (3, 0) else QUARTER
+            for first in range(0, QUARTER, count):
+                if (t, hf) == (0, 1):
+                    picked = early[:, j0 : j0 + QUARTER]
+                else:
+                    picked = windows[t][:].indirect(listed(c * QUARTER + first, count))
+                nc.vector.tensor_tensor(sums[hf][:, t, j0 + first : j0 + first + count], picked,
+                                        y_pairs[c, t // 2][:, t % 2, first : first + count], ADD)
+                if t == 3:
+                    round_pair(1, c, first, count)
             if (t, c) == (1, 1):
                 round_pair(0, 0)
-            if t == 3 or (t == 1 and c > 0):
-                round_pair(t // 2, c)
-            if c % 2 == 1 and t >= 1:
-                done = slice(0, 2) if t == 1 else slice(t, t + 1)
+            if t == 1 and c > 0:
+                round_pair(0, c)
+            if c % 2 == 1 and t >= 2:
+                done = slice(0, 3) if t == 2 else slice(3, 4)
                 nc.sync.dma_start(out_slices[:, done, hf * HALF : (hf + 1) * HALF], sums[hf][:, done, :])
 
         for c in range(4):

@@ -51,20 +51,20 @@ def tile_list_gmlpt_sigm_resLP_kernel(
         def listed(first, count):
             return offsets[:, first // 16 : (first + count) // 16]
 
-        table_rows = keep.tile([P, T], U8, name="table_rows", align_bytes=64)
-        weight_rows = shared.tile([P, 2 * R + N], U8, name="weight_rows", align_bytes=64, offset=LANDING_BYTES)
+        table_rows = keep.tile([P, T + 4], U8, name="table_rows", align_bytes=64)
+        weight_rows = shared.tile([P, 2 * R + N + 4], U8, name="weight_rows", align_bytes=64, offset=LANDING_BYTES)
         staged = keep.tile([P, SCALE_ROW], U8, name="staged", align_bytes=64)
         planes = keep.tile([P, 2, SCALE_ROW], U8, name="planes", align_bytes=64)
-        nc.vector.memset(weight_rows[:, 2 * R :].bitcast(I32), 0)
-        nc.sync.dma_start(table_rows[0:32].bitcast(I32), tab_scales.rearrange("a b t -> b a t").bitcast(I32))
-        nc.scalar.dma_start(weight_rows[0:32, 0:R].bitcast(I32), wg_scales.rearrange("a b n -> b a n").bitcast(I32))
-        nc.scalar.dma_start(weight_rows[0:32, R : 2 * R].bitcast(I32), wu_scales.rearrange("a b n -> b a n").bitcast(I32))
-        nc.scalar.dma_start(weight_rows[0:32:2, 2 * R :].bitcast(I32), wd_scales[0].bitcast(I32))
+        nc.gpsimd.memset(weight_rows[0:32, 2 * R :].bitcast(I32), 0)
+        nc.sync.dma_start(table_rows[0:32, 0:T].bitcast(I32), tab_scales.rearrange("a b t -> b a t").bitcast(I32))
+        nc.sync.dma_start(weight_rows[0:32, 0:R].bitcast(I32), wg_scales.rearrange("a b n -> b a n").bitcast(I32))
+        nc.sync.dma_start(weight_rows[0:32, R : 2 * R].bitcast(I32), wu_scales.rearrange("a b n -> b a n").bitcast(I32))
+        nc.sync.dma_start(weight_rows[0:32:2, 2 * R : 2 * R + N].bitcast(I32), wd_scales[0].bitcast(I32))
         nc.vector.memset(table_rows[32:64].bitcast(I32), 0)
-        nc.gpsimd.memset(table_rows[64:128].bitcast(I32), 0)
+        nc.gpsimd.memset(table_rows[64:128, 0:T].bitcast(I32), 0)
         nc.gpsimd.memset(planes[:].bitcast(I32), 0)
         for rows in (slice(32, 64), slice(64, 128)):
-            nc.vector.memset(weight_rows[rows, 0 : 2 * R].bitcast(I32), 0)
+            nc.vector.memset(weight_rows[rows].bitcast(I32), 0)
 
         landing = shared.tile([P, LANDING_BYTES], U8, name="landing", align_bytes=64, offset=0)
         wg = [landing[:, 0 : 2 * R], keep.tile([P, 2 * R], U8, name="wg_second", align_bytes=64)[:]]
@@ -74,12 +74,13 @@ def tile_list_gmlpt_sigm_resLP_kernel(
         nc.sync.dma_start(wg[1].bitcast(I32), wg_words[1].bitcast(I32))
 
         nc.gpsimd.tensor_copy(staged[:, WG_SCALES:].rearrange("p (w t c i) -> p w c t i", w=3, t=4, i=16),
-                              weight_rows[:].rearrange("p (w c i t) -> p w c t i", w=3, t=4, i=16))
+                              weight_rows[:, 0 : 2 * R + N].rearrange("p (w c i t) -> p w c t i", w=3, t=4, i=16))
         picked_rows = keep.tile([P, J], U8, name="picked_rows", align_bytes=64)
-        nc.vector.tensor_copy(picked_rows[:], table_rows[:].indirect(offsets[:]))
+        nc.vector.tensor_copy(picked_rows[:], table_rows[:, 0:T].indirect(offsets[:]))
         nc.vector.tensor_copy(staged[0:32, 0:J].bitcast(I32), picked_rows[0:32].bitcast(I32))
-        for q in (0, 2, 1, 3):
-            nc.sync.dma_start(planes[32 * q : 32 * q + 4].bitcast(I32), staged[8 * q : 8 * q + 8].bitcast(I32))
+        for q in range(4):
+            queue = nc.sync if q < 2 else nc.scalar
+            queue.dma_start(planes[32 * q : 32 * q + 4].bitcast(I32), staged[8 * q : 8 * q + 8].bitcast(I32))
 
         wg_dealt = shared.tile([P, 4 * R], U8, name="wg_dealt", align_bytes=64, offset=LANDING_BYTES)
         for a in range(2):
@@ -211,8 +212,8 @@ def tile_list_gmlpt_sigm_resLP_kernel(
                 round_pair(0, 0)
             if t == 1 and c > 0:
                 round_pair(0, c)
-            if c % 2 == 1 and t >= 2:
-                done = slice(0, 3) if t == 2 else slice(3, 4)
+            if c % 2 == 1 and t >= 1:
+                done = slice(0, 2) if t == 1 else slice(t, t + 1)
                 nc.sync.dma_start(out_slices[:, done, hf * HALF : (hf + 1) * HALF], sums[hf][:, done, :])
 
         for c in range(4):

@@ -149,7 +149,7 @@ def tile_list_gmlpt_sigm_resLP_kernel(
                             out=ga[:, e, :], lhsT=wg_dealt[:, 2 * c0 : 2 * (c0 + P)].bitcast(FP4X4),
                             lhsT_scale=planes[:, a, WG_SCALES + t * P : WG_SCALES + (t + 1) * P],
                             start=(a == 0), stop=(a == 1), **table_operand(a, c * QUARTER, QUARTER))
-                nc.scalar.activation(gate[:, u, :].rearrange("p (j e) -> p j e", e=2), ga[:].rearrange("p e j -> p j e"), SIGMOID)
+                nc.scalar.activation(gate[:, 2 * u : 2 * u + 2, :], ga[:], SIGMOID)
 
         def gated(c, s, gate, h):
             ub = psum.tile([P, 4, P], F32, name="ub", bufs=2)
@@ -160,9 +160,9 @@ def tile_list_gmlpt_sigm_resLP_kernel(
                         out=ub[:, t, :], lhsT=wu_dealt[:, c0 : c0 + P].bitcast(FP8X4),
                         lhsT_scale=planes[:, a, WU_SCALES + t * P : WU_SCALES + (t + 1) * P],
                         start=(a == 0), stop=(a == 1), **table_operand(a, c * QUARTER + s * P, P))
-            nc.vector.tensor_tensor(h[:, 4 * s * P : 4 * (s + 1) * P].rearrange("p (j u e) -> p j u e", u=2, e=2),
-                                    ub[:].rearrange("p (u e) j -> p j u e", u=2),
-                                    gate[:, :, 2 * s * P : 2 * (s + 1) * P].rearrange("p u (j e) -> p j u e", e=2), MULT)
+            nc.vector.tensor_tensor(h[:, 4 * s * P : 4 * (s + 1) * P].rearrange("p (c i t) -> p c t i", i=2, t=4),
+                                    ub[:].rearrange("p t (c i) -> p c t i", i=2),
+                                    gate[:, :, s * P : (s + 1) * P].rearrange("p t (c i) -> p c t i", i=2), MULT)
 
         def quantise(c, h):
             if c == LAST:
@@ -207,7 +207,9 @@ def tile_list_gmlpt_sigm_resLP_kernel(
                 nc.vector.tensor_tensor(sums[hf][:, t, j0 + first : j0 + first + count], picked,
                                         y_pairs[c, t // 2][:, t % 2, first : first + count], ADD)
                 if t == 3:
-                    round_pair(1, c, first, count)
+                    piece = P if c == LAST else count
+                    for at in range(first, first + count, piece):
+                        round_pair(1, c, at, piece)
             if (t, c) == (1, 1):
                 round_pair(0, 0)
             if t == 1 and c > 0:
@@ -218,7 +220,7 @@ def tile_list_gmlpt_sigm_resLP_kernel(
 
         for c in range(4):
             h = ring.tile([P, 4 * QUARTER], BF16, name="h", align_bytes=64)
-            gate = ring.tile([P, 2, 2 * QUARTER], F32, name="gate", align_bytes=64)
+            gate = ring.tile([P, 4, QUARTER], F32, name="gate", align_bytes=64)
             gates(c, gate)
             for s in range(2):
                 gated(c, s, gate, h)
@@ -244,8 +246,11 @@ def tile_list_gmlpt_sigm_resLP_kernel(
         code_rows = out_1[0].rearrange("p j b -> p (j b)").bitcast(I32)
         for c in range(4):
             span = slice(c * QUARTER, (c + 1) * QUARTER)
-            nc.vector.quantize_mx(out=out_codes[:, span].bitcast(FP8X4), scales=out_scales[:, span],
-                                  in_=rounded[c][:].rearrange("p j t -> p (j t)"))
+            piece = P if c == LAST else QUARTER
+            for at in range(0, QUARTER, piece):
+                part = slice(c * QUARTER + at, c * QUARTER + at + piece)
+                nc.vector.quantize_mx(out=out_codes[:, part].bitcast(FP8X4), scales=out_scales[:, part],
+                                      in_=rounded[c][:, at : at + piece, :].rearrange("p j t -> p (j t)"))
             if c > 0:
                 done = slice(0, HALF) if c == 1 else span
                 nc.sync.dma_start(code_rows[:, done], out_codes[:, done])

@@ -46,7 +46,6 @@ def tile_list_gmlpt_sigm_resLP_kernel(
         shared = ctx.enter_context(tc.tile_pool(name="shared", bufs=1))
 
         offsets = keep.tile([P, J // 16], U16, name="offsets")
-        nc.sync.dma_start(offsets[:], offs)
 
         def listed(first, count):
             return offsets[:, first // 16 : (first + count) // 16]
@@ -57,35 +56,41 @@ def tile_list_gmlpt_sigm_resLP_kernel(
         planes = keep.tile([P, 2, SCALE_ROW], U8, name="planes", align_bytes=64)
         nc.gpsimd.memset(weight_rows[0:32, 2 * R :].bitcast(I32), 0)
         nc.sync.dma_start(table_rows[0:32, 0:T].bitcast(I32), tab_scales.rearrange("a b t -> b a t").bitcast(I32))
+        nc.sync.dma_start(offsets[:], offs)
         nc.sync.dma_start(weight_rows[0:32, 0:R].bitcast(I32), wg_scales.rearrange("a b n -> b a n").bitcast(I32))
+        landing = shared.tile([P, LANDING_BYTES], U8, name="landing", align_bytes=64, offset=0)
+        nc.sync.dma_start(landing[:, 0 : 2 * R].bitcast(I32), wg_words[0].bitcast(I32))
         nc.sync.dma_start(weight_rows[0:32, R : 2 * R].bitcast(I32), wu_scales.rearrange("a b n -> b a n").bitcast(I32))
         nc.sync.dma_start(weight_rows[0:32:2, 2 * R : 2 * R + N].bitcast(I32), wd_scales[0].bitcast(I32))
         nc.vector.memset(table_rows[32:64].bitcast(I32), 0)
         nc.gpsimd.memset(table_rows[64:128, 0:T].bitcast(I32), 0)
-        nc.gpsimd.memset(planes[:].bitcast(I32), 0)
+        plane_bytes = planes[:].rearrange("p a x -> p (a x)")
+        nc.gpsimd.memset(plane_bytes[:, 2 * R :].bitcast(I32), 0)
         for rows in (slice(32, 64), slice(64, 128)):
             nc.vector.memset(weight_rows[rows].bitcast(I32), 0)
 
-        landing = shared.tile([P, LANDING_BYTES], U8, name="landing", align_bytes=64, offset=0)
-        wg = [landing[:, 0 : 2 * R], keep.tile([P, 2 * R], U8, name="wg_second", align_bytes=64)[:]]
+        wg = [landing[:, 0 : 2 * R], plane_bytes[:, 0 : 2 * R]]
         table = keep.tile([P, T], I32, name="table", align_bytes=64)
-        nc.sync.dma_start(wg[0].bitcast(I32), wg_words[0].bitcast(I32))
-        nc.sync.dma_start(table[:], tab_words[0].rearrange("p t b -> p (t b)").bitcast(I32))
         nc.sync.dma_start(wg[1].bitcast(I32), wg_words[1].bitcast(I32))
+        nc.sync.dma_start(table[:], tab_words[0].rearrange("p t b -> p (t b)").bitcast(I32))
 
         nc.gpsimd.tensor_copy(staged[:, WG_SCALES:].rearrange("p (w t c i) -> p w c t i", w=3, t=4, i=16),
                               weight_rows[:, 0 : 2 * R + N].rearrange("p (w c i t) -> p w c t i", w=3, t=4, i=16))
         picked_rows = keep.tile([P, J], U8, name="picked_rows", align_bytes=64)
         nc.vector.tensor_copy(picked_rows[:], table_rows[:, 0:T].indirect(offsets[:]))
         nc.vector.tensor_copy(staged[0:32, 0:J].bitcast(I32), picked_rows[0:32].bitcast(I32))
+        wg_dealt = shared.tile([P, 4 * R], U8, name="wg_dealt", align_bytes=64, offset=LANDING_BYTES)
+
+        def deal_wg(a):
+            nc.vector.tensor_copy(wg_dealt[:, 2 * a * R : 2 * (a + 1) * R].bitcast(U16).rearrange("p (t c i) -> p c t i", t=4, i=8),
+                                  wg[a].bitcast(U16).rearrange("p (c i t) -> p c t i", t=4, i=8))
+
+        deal_wg(1)
         for q in range(4):
             queue = nc.sync if q < 2 else nc.scalar
             queue.dma_start(planes[32 * q : 32 * q + 4].bitcast(I32), staged[8 * q : 8 * q + 8].bitcast(I32))
 
-        wg_dealt = shared.tile([P, 4 * R], U8, name="wg_dealt", align_bytes=64, offset=LANDING_BYTES)
-        for a in range(2):
-            nc.vector.tensor_copy(wg_dealt[:, 2 * a * R : 2 * (a + 1) * R].bitcast(U16).rearrange("p (t c i) -> p c t i", t=4, i=8),
-                                  wg[a].bitcast(U16).rearrange("p (c i t) -> p c t i", t=4, i=8))
+        deal_wg(0)
 
         wu = shared.tile([P, 2 * R], I32, name="wu", align_bytes=64, offset=WU_AT)
         nc.sync.dma_start(wu[:].rearrange("p (a n) -> p a n", a=2), wu_words.rearrange("a p n i -> p a (n i)").bitcast(I32))

@@ -21,16 +21,17 @@ P = 128
 HALF = 512
 QUARTER = 256
 LAST = J // QUARTER - 1
+SPARE = 4
 KB = 1024
 
-WG_SCALES, WU_SCALES, WD_SCALES, SCALE_ROW = J, J + R, J + 2 * R, J + 2 * R + N
+WG_SCALES, WU_SCALES, WD_SCALES, SCALE_ROW = J, J + R, J + 2 * R, J + 2 * R + N // 2
 
 WU_AT = 2 * KB
 WD_AT = 6 * KB
 WINDOWS_AT = 8 * KB
 LANDING_BYTES = WINDOWS_AT + 4 * 4 * T
 ROUNDED_AT = LANDING_BYTES + 3 * KB
-WU_DEALT_AT = 93 * KB
+WU_DEALT_AT = ROUNDED_AT + 8 * KB
 PICKED_AT = WU_DEALT_AT + 3 * KB
 
 
@@ -50,18 +51,16 @@ def tile_list_gmlpt_sigm_resLP_kernel(
         def listed(first, count):
             return offsets[:, first // 16 : (first + count) // 16]
 
-        table_rows = keep.tile([P, T + 4], U8, name="table_rows", align_bytes=64)
-        weight_rows = shared.tile([P, 2 * R + N + 4], U8, name="weight_rows", align_bytes=64, offset=LANDING_BYTES)
+        table_rows = keep.tile([P, T + SPARE], U8, name="table_rows", align_bytes=64)
+        weight_rows = shared.tile([P, 2 * R + SPARE], U8, name="weight_rows", align_bytes=64, offset=LANDING_BYTES)
         staged = keep.tile([P, SCALE_ROW], U8, name="staged", align_bytes=64)
         planes = keep.tile([P, 2, SCALE_ROW], U8, name="planes", align_bytes=64)
-        nc.gpsimd.memset(weight_rows[0:32, 2 * R :].bitcast(I32), 0)
         nc.sync.dma_start(table_rows[0:32, 0:T].bitcast(I32), tab_scales.rearrange("a b t -> b a t").bitcast(I32))
         nc.sync.dma_start(offsets[:], offs)
-        nc.sync.dma_start(weight_rows[0:32, 0:R].bitcast(I32), wg_scales.rearrange("a b n -> b a n").bitcast(I32))
+        nc.sync.dma_start(staged[0:32, WD_SCALES:].bitcast(I32), wd_scales[0].rearrange("b (a n) -> (b a) n", a=2).bitcast(I32))
         landing = shared.tile([P, LANDING_BYTES], U8, name="landing", align_bytes=64, offset=0)
         nc.sync.dma_start(landing[:, 0 : 2 * R].bitcast(I32), wg_words[0].bitcast(I32))
-        nc.sync.dma_start(weight_rows[0:32, R : 2 * R].bitcast(I32), wu_scales.rearrange("a b n -> b a n").bitcast(I32))
-        nc.sync.dma_start(weight_rows[0:32:2, 2 * R : 2 * R + N].bitcast(I32), wd_scales[0].bitcast(I32))
+        nc.sync.dma_start(weight_rows[0:32, 0:R].bitcast(I32), wg_scales.rearrange("a b n -> b a n").bitcast(I32))
         nc.vector.memset(table_rows[32:64].bitcast(I32), 0)
         nc.gpsimd.memset(table_rows[64:128, 0:T].bitcast(I32), 0)
         plane_bytes = planes[:].rearrange("p a x -> p (a x)")
@@ -72,10 +71,11 @@ def tile_list_gmlpt_sigm_resLP_kernel(
         wg = [landing[:, 0 : 2 * R], plane_bytes[:, 0 : 2 * R]]
         table = keep.tile([P, T], I32, name="table", align_bytes=64)
         nc.sync.dma_start(wg[1].bitcast(I32), wg_words[1].bitcast(I32))
+        nc.sync.dma_start(weight_rows[0:32, R : 2 * R].bitcast(I32), wu_scales.rearrange("a b n -> b a n").bitcast(I32))
         nc.sync.dma_start(table[:], tab_words[0].rearrange("p t b -> p (t b)").bitcast(I32))
 
-        nc.gpsimd.tensor_copy(staged[:, WG_SCALES:].rearrange("p (w t c i) -> p w c t i", w=3, t=4, i=16),
-                              weight_rows[:, 0 : 2 * R + N].rearrange("p (w c i t) -> p w c t i", w=3, t=4, i=16))
+        nc.gpsimd.tensor_copy(staged[:, WG_SCALES:WD_SCALES].rearrange("p (w t c i) -> p w c t i", w=2, t=4, i=16),
+                              weight_rows[:, 0 : 2 * R].rearrange("p (w c i t) -> p w c t i", w=2, t=4, i=16))
         picked_rows = keep.tile([P, J], U8, name="picked_rows", align_bytes=64)
         nc.vector.tensor_copy(picked_rows[:], table_rows[:, 0:T].indirect(offsets[:]))
         nc.vector.tensor_copy(staged[0:32, 0:J].bitcast(I32), picked_rows[0:32].bitcast(I32))
@@ -89,15 +89,15 @@ def tile_list_gmlpt_sigm_resLP_kernel(
         for q in range(4):
             queue = nc.sync if q < 2 else nc.scalar
             queue.dma_start(planes[32 * q : 32 * q + 4].bitcast(I32), staged[8 * q : 8 * q + 8].bitcast(I32))
-
         deal_wg(0)
 
         wu = shared.tile([P, 2 * R], I32, name="wu", align_bytes=64, offset=WU_AT)
         nc.sync.dma_start(wu[:].rearrange("p (a n) -> p a n", a=2), wu_words.rearrange("a p n i -> p a (n i)").bitcast(I32))
 
         warm = psum.tile([P, R], F32, name="warm", tag="y", bufs=3)
-        for stationary in 4 * [wg_dealt[:, 0 : 2 * P].bitcast(FP4X4)]:
-            nc.tensor.matmul_mx(out=warm[:], lhsT=stationary, lhsT_scale=staged[:, WG_SCALES : WG_SCALES + P],
+        for warm_pass in range(4):
+            nc.tensor.matmul_mx(out=warm[:], lhsT=wg_dealt[:, 0 : 2 * P].bitcast(FP4X4),
+                                lhsT_scale=staged[:, WG_SCALES : WG_SCALES + P],
                                 rhs=wg_dealt[:, 0 : 2 * R].bitcast(FP4X4), rhs_scale=staged[:, WG_SCALES : WG_SCALES + R],
                                 start=True, stop=True)
 
@@ -132,6 +132,9 @@ def tile_list_gmlpt_sigm_resLP_kernel(
         wd_dealt = keep.tile([P, N], I32, name="wd_dealt", align_bytes=64)
         nc.vector.tensor_copy(wd_dealt[:].rearrange("p (t c i) -> p c t i", t=4, i=4),
                               wd[:].rearrange("p (c i t) -> p c t i", t=4, i=4))
+        wd_plane = keep.tile([P, N], U8, name="wd_plane", align_bytes=64)
+        nc.vector.tensor_copy(wd_plane[:].rearrange("p (t a c i) -> p a c t i", t=4, a=2, i=16),
+                              planes[:, :, WD_SCALES:].rearrange("p a (c i t) -> p a c t i", t=4, i=16))
 
         first_half = keep.tile([P, 4, HALF], F32, name="first_half", align_bytes=64)
         second_half = keep.tile([P, 4 * HALF + 2 * QUARTER], F32, name="second_half", align_bytes=64)
@@ -186,7 +189,7 @@ def tile_list_gmlpt_sigm_resLP_kernel(
                 for e in range(2):
                     t = 2 * u + e
                     nc.tensor.matmul_mx(out=y[:, e, :], lhsT=wd_dealt[:, t * P : (t + 1) * P].bitcast(FP8X4),
-                                        lhsT_scale=planes[:, 0, WD_SCALES + t * P : WD_SCALES + (t + 1) * P],
+                                        lhsT_scale=wd_plane[:, t * P : (t + 1) * P],
                                         rhs=h_codes.bitcast(FP8X4), rhs_scale=h_scales[:], start=True, stop=True)
                 if (c, u) not in y_pairs:
                     y_pairs[c, u] = keep.tile([P, 2, QUARTER], F32, name=f"y_pair{c}{u}", align_bytes=64)[:]
@@ -206,10 +209,10 @@ def tile_list_gmlpt_sigm_resLP_kernel(
             count = P if (t, c) == (3, 0) else QUARTER
             for first in range(0, QUARTER, count):
                 if (t, hf) == (0, 1):
-                    picked = early[:, j0 : j0 + QUARTER]
+                    residual = early[:, j0 : j0 + QUARTER]
                 else:
-                    picked = windows[t][:].indirect(listed(c * QUARTER + first, count))
-                nc.vector.tensor_tensor(sums[hf][:, t, j0 + first : j0 + first + count], picked,
+                    residual = windows[t][:].indirect(listed(c * QUARTER + first, count))
+                nc.vector.tensor_tensor(sums[hf][:, t, j0 + first : j0 + first + count], residual,
                                         y_pairs[c, t // 2][:, t % 2, first : first + count], ADD)
                 if t == 3:
                     piece = P if c == LAST else count

@@ -178,19 +178,24 @@ def tile_list_gmlpt_sigm_resLP_kernel(
             else:
                 h_codes = ring.tile([P, QUARTER], I32, name="h_codes", align_bytes=64)[:]
             h_scales = ring.tile([P, QUARTER], U8, name="h_scales", align_bytes=64)
-            nc.vector.quantize_mx(out=h_codes.bitcast(FP8X4), scales=h_scales[:], in_=h[:])
+            for at in range(0, QUARTER, P):
+                nc.vector.quantize_mx(out=h_codes[:, at : at + P].bitcast(FP8X4), scales=h_scales[:, at : at + P],
+                                      in_=h[:, 4 * at : 4 * (at + P)])
             return h_codes, h_scales
 
         y_pairs = {(1, 1): quarter_rows[:, 3:9:5, :], (2, 1): quarter_rows[:, 1:10:8, :]}
 
         def second_stage(c, h_codes, h_scales):
-            for u in range(2):
-                y = psum.tile([P, 2, QUARTER], F32, name="y", bufs=3)
-                for e in range(2):
-                    t = 2 * u + e
-                    nc.tensor.matmul_mx(out=y[:, e, :], lhsT=wd_dealt[:, t * P : (t + 1) * P].bitcast(FP8X4),
+            banks = [psum.tile([P, 2, QUARTER], F32, name="y", bufs=3) for u in range(2)]
+            piece = P if c == LAST else QUARTER
+            for at in range(0, QUARTER, piece):
+                for t in range(4):
+                    nc.tensor.matmul_mx(out=banks[t // 2][:, t % 2, at : at + piece],
+                                        lhsT=wd_dealt[:, t * P : (t + 1) * P].bitcast(FP8X4),
                                         lhsT_scale=wd_plane[:, t * P : (t + 1) * P],
-                                        rhs=h_codes.bitcast(FP8X4), rhs_scale=h_scales[:], start=True, stop=True)
+                                        rhs=h_codes[:, at : at + piece].bitcast(FP8X4),
+                                        rhs_scale=h_scales[:, at : at + piece], start=True, stop=True)
+            for u, y in enumerate(banks):
                 if (c, u) not in y_pairs:
                     y_pairs[c, u] = keep.tile([P, 2, QUARTER], F32, name=f"y_pair{c}{u}", align_bytes=64)[:]
                 nc.scalar.copy(y_pairs[c, u], y[:])
@@ -201,8 +206,9 @@ def tile_list_gmlpt_sigm_resLP_kernel(
 
         def round_pair(u, c, first=0, count=QUARTER):
             hf, j0 = divmod(c * QUARTER + first, HALF)
-            nc.scalar.copy(rounded[c][:, first : first + count, 2 * u : 2 * u + 2],
-                           sums[hf][:, 2 * u : 2 * u + 2, j0 : j0 + count].rearrange("p e j -> p j e"))
+            copy = nc.vector.tensor_copy if (u, c, first) == (1, LAST - 1, P) else nc.scalar.copy
+            copy(rounded[c][:, first : first + count, 2 * u : 2 * u + 2],
+                 sums[hf][:, 2 * u : 2 * u + 2, j0 : j0 + count].rearrange("p e j -> p j e"))
 
         def add_residual(t, c):
             hf, j0 = divmod(c * QUARTER, HALF)
@@ -215,7 +221,7 @@ def tile_list_gmlpt_sigm_resLP_kernel(
                 nc.vector.tensor_tensor(sums[hf][:, t, j0 + first : j0 + first + count], residual,
                                         y_pairs[c, t // 2][:, t % 2, first : first + count], ADD)
                 if t == 3:
-                    piece = P if c == LAST else count
+                    piece = P if c >= LAST - 1 else count
                     for at in range(first, first + count, piece):
                         round_pair(1, c, at, piece)
             if (t, c) == (1, 1):
@@ -252,16 +258,16 @@ def tile_list_gmlpt_sigm_resLP_kernel(
         out_codes = keep.tile([P, J], I32, name="out_codes", align_bytes=64)
         out_scales = keep.tile([P, J], U8, name="out_scales", align_bytes=64)
         code_rows = out_1[0].rearrange("p j b -> p (j b)").bitcast(I32)
+        stored = 0
         for c in range(4):
-            span = slice(c * QUARTER, (c + 1) * QUARTER)
             piece = P if c == LAST else QUARTER
             for at in range(0, QUARTER, piece):
                 part = slice(c * QUARTER + at, c * QUARTER + at + piece)
                 nc.vector.quantize_mx(out=out_codes[:, part].bitcast(FP8X4), scales=out_scales[:, part],
                                       in_=rounded[c][:, at : at + piece, :].rearrange("p j t -> p (j t)"))
-            if c > 0:
-                done = slice(0, HALF) if c == 1 else span
-                nc.sync.dma_start(code_rows[:, done], out_codes[:, done])
+                if c % 2 == 1:
+                    nc.sync.dma_start(code_rows[:, stored : part.stop], out_codes[:, stored : part.stop])
+                    stored = part.stop
         for q in range(4):
             queue = nc.sync if q % 2 == 0 else nc.scalar
             queue.dma_start(out_2[0, 4 * q : 4 * q + 4, :].bitcast(I32), out_scales[32 * q : 32 * q + 4].bitcast(I32))

@@ -30,8 +30,7 @@ WU_AT = 2 * KB
 WD_AT = 6 * KB
 WINDOWS_AT = 8 * KB
 LANDING_BYTES = WINDOWS_AT + 4 * 4 * T
-ROUNDED_AT = LANDING_BYTES + 3 * KB
-WU_DEALT_AT = ROUNDED_AT + 8 * KB
+WU_DEALT_AT = LANDING_BYTES + 3 * KB
 PICKED_AT = WU_DEALT_AT + 3 * KB
 
 
@@ -136,10 +135,7 @@ def tile_list_gmlpt_sigm_resLP_kernel(
         nc.vector.tensor_copy(wd_plane[:].rearrange("p (t a c i) -> p a c t i", t=4, a=2, i=16),
                               planes[:, :, WD_SCALES:].rearrange("p a (c i t) -> p a c t i", t=4, i=16))
 
-        first_half = keep.tile([P, 4, HALF], F32, name="first_half", align_bytes=64)
-        second_half = keep.tile([P, 4 * HALF + 2 * QUARTER], F32, name="second_half", align_bytes=64)
-        sums = [first_half[:], second_half[:, 0 : 4 * HALF].rearrange("p (t j) -> p t j", t=4)]
-        quarter_rows = second_half[:].rearrange("p (e x) -> p e x", x=QUARTER)
+        sums = keep.tile([P, 4, J], F32, name="sums", align_bytes=64)
 
         def table_operand(a, first, count):
             hf, j0 = divmod(first, HALF)
@@ -172,18 +168,15 @@ def tile_list_gmlpt_sigm_resLP_kernel(
                                     ub[:].rearrange("p t (c i) -> p c t i", i=2),
                                     gate[:, :, s * P : (s + 1) * P].rearrange("p t (c i) -> p c t i", i=2), MULT)
 
-        def quantise(c, h):
-            if c == LAST:
-                h_codes = shared.tile([P, 4 * QUARTER], I32, name="h_codes_wide", align_bytes=64, offset=ROUNDED_AT)[:, 0:QUARTER]
-            else:
-                h_codes = ring.tile([P, QUARTER], I32, name="h_codes", align_bytes=64)[:]
+        def quantise(h):
+            h_codes = ring.tile([P, QUARTER], I32, name="h_codes", align_bytes=64)
             h_scales = ring.tile([P, QUARTER], U8, name="h_scales", align_bytes=64)
             for at in range(0, QUARTER, P):
                 nc.vector.quantize_mx(out=h_codes[:, at : at + P].bitcast(FP8X4), scales=h_scales[:, at : at + P],
                                       in_=h[:, 4 * at : 4 * (at + P)])
             return h_codes, h_scales
 
-        y_pairs = {(1, 1): quarter_rows[:, 3:9:5, :], (2, 1): quarter_rows[:, 1:10:8, :]}
+        ys = keep.tile([P, 4, J], F32, name="ys", align_bytes=64)
 
         def second_stage(c, h_codes, h_scales):
             banks = [psum.tile([P, 2, QUARTER], F32, name="y", bufs=3) for u in range(2)]
@@ -196,41 +189,19 @@ def tile_list_gmlpt_sigm_resLP_kernel(
                                         rhs=h_codes[:, at : at + piece].bitcast(FP8X4),
                                         rhs_scale=h_scales[:, at : at + piece], start=True, stop=True)
             for u, y in enumerate(banks):
-                if (c, u) not in y_pairs:
-                    y_pairs[c, u] = keep.tile([P, 2, QUARTER], F32, name=f"y_pair{c}{u}", align_bytes=64)[:]
-                nc.scalar.copy(y_pairs[c, u], y[:])
+                nc.scalar.copy(ys[:, 2 * u : 2 * u + 2, c * QUARTER : (c + 1) * QUARTER], y[:])
 
         out_slices = out_0.rearrange("(p t) j -> p t j", t=4)
-        rounded = [shared.tile([P, QUARTER, 4], BF16, name=f"rounded{c}", align_bytes=64, offset=ROUNDED_AT + 2 * c * KB)
-                   for c in range(4)]
+        rounded = keep.tile([P, J, 4], BF16, name="rounded", align_bytes=64)
 
-        def round_pair(u, c, first=0, count=QUARTER):
-            hf, j0 = divmod(c * QUARTER + first, HALF)
-            copy = nc.vector.tensor_copy if (u, c, first) == (1, LAST - 1, P) else nc.scalar.copy
-            copy(rounded[c][:, first : first + count, 2 * u : 2 * u + 2],
-                 sums[hf][:, 2 * u : 2 * u + 2, j0 : j0 + count].rearrange("p e j -> p j e"))
+        def round_pair(copy, u, first, count):
+            copy(rounded[:, first : first + count, 2 * u : 2 * u + 2],
+                 sums[:, 2 * u : 2 * u + 2, first : first + count].rearrange("p e j -> p j e"))
 
-        def add_residual(t, c):
-            hf, j0 = divmod(c * QUARTER, HALF)
-            count = P if (t, c) == (3, 0) else QUARTER
-            for first in range(0, QUARTER, count):
-                if (t, hf) == (0, 1):
-                    residual = early[:, j0 : j0 + QUARTER]
-                else:
-                    residual = windows[t][:].indirect(listed(c * QUARTER + first, count))
-                nc.vector.tensor_tensor(sums[hf][:, t, j0 + first : j0 + first + count], residual,
-                                        y_pairs[c, t // 2][:, t % 2, first : first + count], ADD)
-                if t == 3:
-                    piece = P if c >= LAST - 1 else count
-                    for at in range(first, first + count, piece):
-                        round_pair(1, c, at, piece)
-            if (t, c) == (1, 1):
-                round_pair(0, 0)
-            if t == 1 and c > 0:
-                round_pair(0, c)
-            if c % 2 == 1 and t >= 1:
-                done = slice(0, 2) if t == 1 else slice(t, t + 1)
-                nc.sync.dma_start(out_slices[:, done, hf * HALF : (hf + 1) * HALF], sums[hf][:, done, :])
+        def add_residual(t, first, count, residual=None):
+            if residual is None:
+                residual = windows[t][:].indirect(listed(first, count))
+            nc.vector.tensor_tensor(sums[:, t, first : first + count], residual, ys[:, t, first : first + count], ADD)
 
         for c in range(4):
             h = ring.tile([P, 4 * QUARTER], BF16, name="h", align_bytes=64)
@@ -240,34 +211,41 @@ def tile_list_gmlpt_sigm_resLP_kernel(
                 gated(c, s, gate, h)
             if c > 0:
                 second_stage(c - 1, *quantised)
-            quantised = quantise(c, h)
+            quantised = quantise(h)
         second_stage(LAST, *quantised)
 
         early = keep.tile([P, HALF], F32, name="early", align_bytes=64)
         nc.vector.tensor_copy(early[:], windows[0][:].indirect(listed(HALF, HALF)))
-        for c in range(LAST):
-            for t in range(2):
-                add_residual(t, c)
-        for c in range(LAST):
-            add_residual(2, c)
-        for t in range(3):
-            add_residual(t, LAST)
-        for c in range(4):
-            add_residual(3, c)
+        for first in range(0, J, QUARTER):
+            add_residual(0, first, QUARTER, early[:, first - HALF : first - HALF + QUARTER] if first >= HALF else None)
+            if first == LAST * QUARTER:
+                round_pair(nc.scalar.copy, 0, 0, first)
+            add_residual(1, first, QUARTER)
+        round_pair(nc.scalar.copy, 0, LAST * QUARTER, QUARTER)
+        nc.sync.dma_start(out_slices[:, 0:2, :], sums[:, 0:2, :])
+        for first in range(0, J, HALF):
+            add_residual(2, first, HALF)
+        nc.sync.dma_start(out_slices[:, 2, :], sums[:, 2, :])
+        for first, count in ((0, P), (P, P), (QUARTER, QUARTER), (HALF, QUARTER), (LAST * QUARTER, QUARTER)):
+            add_residual(3, first, count)
+            piece = P if first >= HALF else count
+            for at in range(first, first + count, piece):
+                round_pair(nc.vector.tensor_copy if at == HALF + P else nc.scalar.copy, 1, at, piece)
+            if (first + count) % HALF == 0:
+                half = slice(first + count - HALF, first + count)
+                nc.sync.dma_start(out_slices[:, 3, half], sums[:, 3, half])
 
         out_codes = keep.tile([P, J], I32, name="out_codes", align_bytes=64)
         out_scales = keep.tile([P, J], U8, name="out_scales", align_bytes=64)
         code_rows = out_1[0].rearrange("p j b -> p (j b)").bitcast(I32)
         stored = 0
-        for c in range(4):
-            piece = P if c == LAST else QUARTER
-            for at in range(0, QUARTER, piece):
-                part = slice(c * QUARTER + at, c * QUARTER + at + piece)
-                nc.vector.quantize_mx(out=out_codes[:, part].bitcast(FP8X4), scales=out_scales[:, part],
-                                      in_=rounded[c][:, at : at + piece, :].rearrange("p j t -> p (j t)"))
-                if c % 2 == 1:
-                    nc.sync.dma_start(code_rows[:, stored : part.stop], out_codes[:, stored : part.stop])
-                    stored = part.stop
+        for first, count in ((0, HALF), (HALF, QUARTER), (LAST * QUARTER, P), (J - P, P)):
+            part = slice(first, first + count)
+            nc.vector.quantize_mx(out=out_codes[:, part].bitcast(FP8X4), scales=out_scales[:, part],
+                                  in_=rounded[:, part, :].rearrange("p j t -> p (j t)"))
+            if count != QUARTER:
+                nc.sync.dma_start(code_rows[:, stored : part.stop], out_codes[:, stored : part.stop])
+                stored = part.stop
         for q in range(4):
             queue = nc.sync if q % 2 == 0 else nc.scalar
             queue.dma_start(out_2[0, 4 * q : 4 * q + 4, :].bitcast(I32), out_scales[32 * q : 32 * q + 4].bitcast(I32))

@@ -93,13 +93,6 @@ def tile_list_gmlpt_sigm_resLP_kernel(
         wu = shared.tile([P, 2 * R], I32, name="wu", align_bytes=64, offset=WU_AT)
         nc.sync.dma_start(wu[:].rearrange("p (a n) -> p a n", a=2), wu_words.rearrange("a p n i -> p a (n i)").bitcast(I32))
 
-        warm = psum.tile([P, R], F32, name="warm", tag="y", bufs=3)
-        for warm_pass in range(4):
-            nc.tensor.matmul_mx(out=warm[:], lhsT=wg_dealt[:, 0 : 2 * P].bitcast(FP4X4),
-                                lhsT_scale=staged[:, WG_SCALES : WG_SCALES + P],
-                                rhs=wg_dealt[:, 0 : 2 * R].bitcast(FP4X4), rhs_scale=staged[:, WG_SCALES : WG_SCALES + R],
-                                start=True, stop=True)
-
         wd = shared.tile([P, N], I32, name="wd", align_bytes=64, offset=WD_AT)
         nc.sync.dma_start(wd[:], wd_words[0].rearrange("p n i -> p (n i)").bitcast(I32))
         r_slices = rT.rearrange("(p t) c -> p t c", t=4)

@@ -102,25 +102,21 @@ def tile_list_gmlpt_sigm_resLP_kernel(
             nc.sync.dma_start(window[:], r_slices[:, t, :])
             windows.append(window)
 
-        parted = []
+        parted = {}
 
-        def pick_words(hf, pieces):
-            picked = shared.tile([P, HALF], U32, name=f"picked{hf}", align_bytes=64, offset=(PICKED_AT, WU_AT)[hf])
-            nc.vector.tensor_copy(picked[:], table[:].bitcast(U32).indirect(listed(hf * HALF, HALF)))
-            words = keep.tile([P, 4 * HALF], U8, name=f"parted{hf}", align_bytes=64)
-            lines = HALF // 8 // pieces
-            for first in range(0, HALF // 8, lines):
-                nc.vector.tensor_copy(
-                    words[:].bitcast(U16).rearrange("p (a c i) -> p c a i", a=2, i=8)[:, first : first + lines],
-                    picked[:].bitcast(U16).rearrange("p (c i a) -> p c a i", a=2, i=8)[:, first : first + lines],
-                )
-            parted.append(words)
+        def pick_words(first, count, picked):
+            nc.vector.tensor_copy(picked[:], table[:].bitcast(U32).indirect(listed(first, count)))
+            words = keep.tile([P, 4 * count], U8, name=f"parted{first}", align_bytes=64)
+            nc.vector.tensor_copy(words[:].bitcast(U16).rearrange("p (a c i) -> p c a i", a=2, i=8),
+                                  picked[:].bitcast(U16).rearrange("p (c i a) -> p c a i", a=2, i=8))
+            parted[first] = (words, count)
 
-        pick_words(0, 2)
+        for first in (0, QUARTER):
+            pick_words(first, QUARTER, shared.tile([P, QUARTER], U32, name="picked", align_bytes=64, offset=PICKED_AT))
         wu_dealt = shared.tile([P, 2 * R], I32, name="wu_dealt", align_bytes=64, offset=WU_DEALT_AT)
         nc.vector.tensor_copy(wu_dealt[:].rearrange("p (a t c i) -> p a c t i", a=2, t=4, i=4),
                               wu[:].rearrange("p (a c i t) -> p a c t i", a=2, t=4, i=4))
-        pick_words(1, 1)
+        pick_words(HALF, HALF, shared.tile([P, HALF], U32, name="picked_half", align_bytes=64, offset=WU_AT))
         wd_dealt = keep.tile([P, N], I32, name="wd_dealt", align_bytes=64)
         nc.vector.tensor_copy(wd_dealt[:].rearrange("p (t c i) -> p c t i", t=4, i=4),
                               wd[:].rearrange("p (c i t) -> p c t i", t=4, i=4))
@@ -131,9 +127,10 @@ def tile_list_gmlpt_sigm_resLP_kernel(
         sums = keep.tile([P, 4, J], F32, name="sums", align_bytes=64)
 
         def table_operand(a, first, count):
-            hf, j0 = divmod(first, HALF)
-            b0 = 2 * (a * HALF + j0)
-            return dict(rhs=parted[hf][:, b0 : b0 + 2 * count].bitcast(FP4X4), rhs_scale=planes[:, a, first : first + count])
+            start = max(at for at in parted if at <= first)
+            words, tokens = parted[start]
+            b0 = 2 * (a * tokens + first - start)
+            return dict(rhs=words[:, b0 : b0 + 2 * count].bitcast(FP4X4), rhs_scale=planes[:, a, first : first + count])
 
         def gates(c, gate):
             for u in range(2):
@@ -170,9 +167,10 @@ def tile_list_gmlpt_sigm_resLP_kernel(
             return h_codes, h_scales
 
         ys = keep.tile([P, 4, J], F32, name="ys", align_bytes=64)
+        in_bank = {}
 
         def second_stage(c, h_codes, h_scales):
-            banks = [psum.tile([P, 2, QUARTER], F32, name="y", bufs=3) for u in range(2)]
+            banks = [psum.tile([P, 2, QUARTER], F32, name="ga" if c == LAST else "y", bufs=3) for u in range(2)]
             piece = P if c == LAST else QUARTER
             for at in range(0, QUARTER, piece):
                 for t in range(4):
@@ -181,8 +179,13 @@ def tile_list_gmlpt_sigm_resLP_kernel(
                                         lhsT_scale=wd_plane[:, t * P : (t + 1) * P],
                                         rhs=h_codes[:, at : at + piece].bitcast(FP8X4),
                                         rhs_scale=h_scales[:, at : at + piece], start=True, stop=True)
-            for u, y in enumerate(banks):
-                nc.scalar.copy(ys[:, 2 * u : 2 * u + 2, c * QUARTER : (c + 1) * QUARTER], y[:])
+            tokens = slice(c * QUARTER, (c + 1) * QUARTER)
+            if tokens.start < HALF:
+                nc.scalar.copy(ys[:, 0:2, tokens], banks[0][:])
+            else:
+                in_bank[tokens.start] = banks[0][:, 0, :]
+                nc.scalar.copy(ys[:, 1, tokens], banks[0][:, 1, :])
+            nc.scalar.copy(ys[:, 2:4, tokens], banks[1][:])
 
         out_slices = out_0.rearrange("(p t) j -> p t j", t=4)
         rounded = keep.tile([P, J, 4], BF16, name="rounded", align_bytes=64)
@@ -191,10 +194,9 @@ def tile_list_gmlpt_sigm_resLP_kernel(
             copy(rounded[:, first : first + count, 2 * u : 2 * u + 2],
                  sums[:, 2 * u : 2 * u + 2, first : first + count].rearrange("p e j -> p j e"))
 
-        def add_residual(t, first, count, residual=None):
-            if residual is None:
-                residual = windows[t][:].indirect(listed(first, count))
-            nc.vector.tensor_tensor(sums[:, t, first : first + count], residual, ys[:, t, first : first + count], ADD)
+        def add_residual(t, first, count):
+            nc.vector.tensor_tensor(sums[:, t, first : first + count], windows[t][:].indirect(listed(first, count)),
+                                    ys[:, t, first : first + count], ADD)
 
         for c in range(4):
             h = ring.tile([P, 4 * QUARTER], BF16, name="h", align_bytes=64)
@@ -210,7 +212,11 @@ def tile_list_gmlpt_sigm_resLP_kernel(
         early = keep.tile([P, HALF], F32, name="early", align_bytes=64)
         nc.vector.tensor_copy(early[:], windows[0][:].indirect(listed(HALF, HALF)))
         for first in range(0, J, QUARTER):
-            add_residual(0, first, QUARTER, early[:, first - HALF : first - HALF + QUARTER] if first >= HALF else None)
+            if first < HALF:
+                add_residual(0, first, QUARTER)
+            else:
+                nc.vector.tensor_tensor(sums[:, 0, first : first + QUARTER], early[:, first - HALF : first - HALF + QUARTER],
+                                        in_bank[first], ADD)
             if first == LAST * QUARTER:
                 round_pair(nc.scalar.copy, 0, 0, first)
             add_residual(1, first, QUARTER)
@@ -239,6 +245,6 @@ def tile_list_gmlpt_sigm_resLP_kernel(
             if count != QUARTER:
                 nc.sync.dma_start(code_rows[:, stored : part.stop], out_codes[:, stored : part.stop])
                 stored = part.stop
-        for q in range(4):
-            queue = nc.sync if q % 2 == 0 else nc.scalar
-            queue.dma_start(out_2[0, 4 * q : 4 * q + 4, :].bitcast(I32), out_scales[32 * q : 32 * q + 4].bitcast(I32))
+        for s in range(4):
+            queue = nc.sync if s % 2 == 0 else nc.scalar
+            queue.dma_start(out_2[0, s:16:4, :].bitcast(I32), out_scales[s:P:32].bitcast(I32))

@@ -225,24 +225,25 @@ def tile_list_gmlpt_sigm_resLP_kernel(
         for first in range(0, J, HALF):
             add_residual(2, first, HALF)
         nc.sync.dma_start(out_slices[:, 2, :], sums[:, 2, :])
-        for first, count in ((0, P), (P, P), (QUARTER, QUARTER), (HALF, QUARTER), (LAST * QUARTER, QUARTER)):
+        stored = 0
+        for first, count in ((0, P), (P, P), (QUARTER, QUARTER), (HALF, P), (HALF + P, P), (LAST * QUARTER, QUARTER)):
             add_residual(3, first, count)
             piece = P if first >= HALF else count
             for at in range(first, first + count, piece):
                 round_pair(nc.vector.tensor_copy if at == HALF + P else nc.scalar.copy, 1, at, piece)
-            if (first + count) % HALF == 0:
-                half = slice(first + count - HALF, first + count)
-                nc.sync.dma_start(out_slices[:, 3, half], sums[:, 3, half])
+            if first + count in (HALF + P, J):
+                nc.sync.dma_start(out_slices[:, 3, stored : first + count], sums[:, 3, stored : first + count])
+                stored = first + count
 
         out_codes = keep.tile([P, J], I32, name="out_codes", align_bytes=64)
         out_scales = keep.tile([P, J], U8, name="out_scales", align_bytes=64)
         code_rows = out_1[0].rearrange("p j b -> p (j b)").bitcast(I32)
         stored = 0
-        for first, count in ((0, HALF), (HALF, QUARTER), (LAST * QUARTER, P), (J - P, P)):
+        for first, count in ((0, QUARTER), (QUARTER, QUARTER), (HALF, QUARTER), (LAST * QUARTER, P), (J - P, P)):
             part = slice(first, first + count)
             nc.vector.quantize_mx(out=out_codes[:, part].bitcast(FP8X4), scales=out_scales[:, part],
                                   in_=rounded[:, part, :].rearrange("p j t -> p (j t)"))
-            if count != QUARTER:
+            if first != HALF:
                 nc.sync.dma_start(code_rows[:, stored : part.stop], out_codes[:, stored : part.stop])
                 stored = part.stop
         for s in range(4):

@@ -90,8 +90,10 @@ def tile_list_gmlpt_sigm_resLP_kernel(
             queue.dma_start(planes[32 * q : 32 * q + 4].bitcast(I32), staged[8 * q : 8 * q + 8].bitcast(I32))
         deal_wg(0)
 
-        wu = shared.tile([P, 2 * R], I32, name="wu", align_bytes=64, offset=WU_AT)
-        nc.sync.dma_start(wu[:].rearrange("p (a n) -> p a n", a=2), wu_words.rearrange("a p n i -> p a (n i)").bitcast(I32))
+        wu = []
+        for a in range(2):
+            wu.append(shared.tile([P, R], I32, name=f"wu{a}", align_bytes=64, offset=WU_AT + a * 4 * R))
+            nc.sync.dma_start(wu[a][:], wu_words[a].rearrange("p n i -> p (n i)").bitcast(I32))
 
         wd = shared.tile([P, N], I32, name="wd", align_bytes=64, offset=WD_AT)
         nc.sync.dma_start(wd[:], wd_words[0].rearrange("p n i -> p (n i)").bitcast(I32))
@@ -114,9 +116,10 @@ def tile_list_gmlpt_sigm_resLP_kernel(
         for first in (0, QUARTER):
             pick_words(first, QUARTER, shared.tile([P, QUARTER], U32, name="picked", align_bytes=64, offset=PICKED_AT))
         wu_dealt = shared.tile([P, 2 * R], I32, name="wu_dealt", align_bytes=64, offset=WU_DEALT_AT)
-        nc.vector.tensor_copy(wu_dealt[:].rearrange("p (a t c i) -> p a c t i", a=2, t=4, i=4),
-                              wu[:].rearrange("p (a c i t) -> p a c t i", a=2, t=4, i=4))
-        pick_words(HALF, HALF, shared.tile([P, HALF], U32, name="picked_half", align_bytes=64, offset=WU_AT))
+        for a in range(2):
+            nc.vector.tensor_copy(wu_dealt[:, a * R : (a + 1) * R].rearrange("p (t c i) -> p c t i", t=4, i=4),
+                                  wu[a][:].rearrange("p (c i t) -> p c t i", t=4, i=4))
+        pick_words(HALF, HALF, shared.tile([P, HALF], U32, name="picked_half", align_bytes=64, offset=WU_AT + 4 * R))
         wd_dealt = keep.tile([P, N], I32, name="wd_dealt", align_bytes=64)
         nc.vector.tensor_copy(wd_dealt[:].rearrange("p (t c i) -> p c t i", t=4, i=4),
                               wd[:].rearrange("p (c i t) -> p c t i", t=4, i=4))

from contextlib import ExitStack

import concourse.mybir as mybir

K, R, N, T, J = 1024, 512, 512, 4096, 1024
FLOPS = 2 * J * (2 * K * R + R * N)

F32 = mybir.dt.float32
BF16 = mybir.dt.bfloat16
I32 = mybir.dt.int32
U32 = mybir.dt.uint32
U16 = mybir.dt.uint16
U8 = mybir.dt.uint8
FP8X4 = mybir.dt.float8_e4m3fn_x4
FP4X4 = mybir.dt.float4_e2m1fn_x4
ADD = mybir.AluOpType.add
MULT = mybir.AluOpType.mult
SIGMOID = mybir.ActivationFunctionType.Sigmoid

P = 128
HALF = 512
QUARTER = 256
LAST = J // QUARTER - 1
SPARE = 4
KB = 1024

WG_SCALES, WU_SCALES, WD_SCALES, SCALE_ROW = J, J + R, J + 2 * R, J + 2 * R + N // 2

WU_AT = 2 * KB
WD_AT = 6 * KB
WINDOWS_AT = 8 * KB
LANDING_BYTES = WINDOWS_AT + 4 * 4 * T
WU_DEALT_AT = LANDING_BYTES + 3 * KB
PICKED_AT = WU_DEALT_AT + 3 * KB


def tile_list_gmlpt_sigm_resLP_kernel(
    tc, tab_words, tab_scales, wg_words, wg_scales, wu_words, wu_scales, wd_words, wd_scales, rT, offs,
    out_0, out_1, out_2,
):
    nc = tc.nc
    with ExitStack() as ctx:
        keep = ctx.enter_context(tc.tile_pool(name="keep", bufs=1))
        ring = ctx.enter_context(tc.tile_pool(name="ring", bufs=4))
        psum = ctx.enter_context(tc.psum_pool(name="psum", bufs=2))
        shared = ctx.enter_context(tc.tile_pool(name="shared", bufs=1))

        offsets = keep.tile([P, J // 16], U16, name="offsets")

        def listed(first, count):
            return offsets[:, first // 16 : (first + count) // 16]

        table_rows = keep.tile([P, T + SPARE], U8, name="table_rows", align_bytes=64)
        weight_rows = shared.tile([P, 2 * R + SPARE], U8, name="weight_rows", align_bytes=64, offset=LANDING_BYTES)
        staged = keep.tile([P, SCALE_ROW], U8, name="staged", align_bytes=64)
        planes = keep.tile([P, 2, SCALE_ROW], U8, name="planes", align_bytes=64)
        nc.sync.dma_start(table_rows[0:32, 0:T].bitcast(I32), tab_scales.rearrange("a b t -> b a t").bitcast(I32))
        nc.sync.dma_start(offsets[:], offs)
        nc.sync.dma_start(staged[0:32, WD_SCALES:].bitcast(I32), wd_scales[0].rearrange("b (a n) -> (b a) n", a=2).bitcast(I32))
        landing = shared.tile([P, LANDING_BYTES], U8, name="landing", align_bytes=64, offset=0)
        nc.sync.dma_start(landing[:, 0 : 2 * R].bitcast(I32), wg_words[0].bitcast(I32))
        nc.sync.dma_start(weight_rows[0:32, 0:R].bitcast(I32), wg_scales.rearrange("a b n -> b a n").bitcast(I32))
        nc.vector.memset(table_rows[32:64].bitcast(I32), 0)
        nc.gpsimd.memset(table_rows[64:128, 0:T].bitcast(I32), 0)
        plane_bytes = planes[:].rearrange("p a x -> p (a x)")
        nc.gpsimd.memset(plane_bytes[:, 2 * R :].bitcast(I32), 0)
        for rows in (slice(32, 64), slice(64, 128)):
            nc.vector.memset(weight_rows[rows].bitcast(I32), 0)

        wg = [landing[:, 0 : 2 * R], plane_bytes[:, 0 : 2 * R]]
        table = keep.tile([P, T], I32, name="table", align_bytes=64)
        nc.sync.dma_start(wg[1].bitcast(I32), wg_words[1].bitcast(I32))
        nc.sync.dma_start(weight_rows[0:32, R : 2 * R].bitcast(I32), wu_scales.rearrange("a b n -> b a n").bitcast(I32))
        nc.sync.dma_start(table[:], tab_words[0].rearrange("p t b -> p (t b)").bitcast(I32))

        nc.gpsimd.tensor_copy(staged[:, WG_SCALES:WD_SCALES].rearrange("p (w t c i) -> p w c t i", w=2, t=4, i=16),
                              weight_rows[:, 0 : 2 * R].rearrange("p (w c i t) -> p w c t i", w=2, t=4, i=16))
        picked_rows = keep.tile([P, J], U8, name="picked_rows", align_bytes=64)
        nc.vector.tensor_copy(picked_rows[:], table_rows[:, 0:T].indirect(offsets[:]))
        nc.vector.tensor_copy(staged[0:32, 0:J].bitcast(I32), picked_rows[0:32].bitcast(I32))
        wg_dealt = shared.tile([P, 4 * R], U8, name="wg_dealt", align_bytes=64, offset=LANDING_BYTES)

        def deal_wg(a):
            nc.vector.tensor_copy(wg_dealt[:, 2 * a * R : 2 * (a + 1) * R].bitcast(U16).rearrange("p (t c i) -> p c t i", t=4, i=8),
                                  wg[a].bitcast(U16).rearrange("p (c i t) -> p c t i", t=4, i=8))

        deal_wg(1)
        for q in range(4):
            queue = nc.sync if q < 2 else nc.scalar
            queue.dma_start(planes[32 * q : 32 * q + 4].bitcast(I32), staged[8 * q : 8 * q + 8].bitcast(I32))
        deal_wg(0)

        wu = []
        for a in range(2):
            wu.append(shared.tile([P, R], I32, name=f"wu{a}", align_bytes=64, offset=WU_AT + a * 4 * R))
            nc.sync.dma_start(wu[a][:], wu_words[a].rearrange("p n i -> p (n i)").bitcast(I32))

        wd = shared.tile([P, N], I32, name="wd", align_bytes=64, offset=WD_AT)
        nc.sync.dma_start(wd[:], wd_words[0].rearrange("p n i -> p (n i)").bitcast(I32))
        r_slices = rT.rearrange("(p t) c -> p t c", t=4)
        windows = []
        for t in range(4):
            window = shared.tile([P, T], F32, name=f"window{t}", align_bytes=64, offset=WINDOWS_AT + t * 4 * T)
            nc.sync.dma_start(window[:], r_slices[:, t, :])
            windows.append(window)

        parted = {}

        def pick_words(first, count, picked):
            nc.vector.tensor_copy(picked[:], table[:].bitcast(U32).indirect(listed(first, count)))
            words = keep.tile([P, 4 * count], U8, name=f"parted{first}", align_bytes=64)
            nc.vector.tensor_copy(words[:].bitcast(U16).rearrange("p (a c i) -> p c a i", a=2, i=8),
                                  picked[:].bitcast(U16).rearrange("p (c i a) -> p c a i", a=2, i=8))
            parted[first] = (words, count)

        for first in (0, QUARTER):
            pick_words(first, QUARTER, shared.tile([P, QUARTER], U32, name="picked", align_bytes=64, offset=PICKED_AT))
        wu_dealt = shared.tile([P, 2 * R], I32, name="wu_dealt", align_bytes=64, offset=WU_DEALT_AT)
        for a in range(2):
            nc.vector.tensor_copy(wu_dealt[:, a * R : (a + 1) * R].rearrange("p (t c i) -> p c t i", t=4, i=4),
                                  wu[a][:].rearrange("p (c i t) -> p c t i", t=4, i=4))
        pick_words(HALF, HALF, shared.tile([P, HALF], U32, name="picked_half", align_bytes=64, offset=WU_AT + 4 * R))
        wd_dealt = keep.tile([P, N], I32, name="wd_dealt", align_bytes=64)
        nc.vector.tensor_copy(wd_dealt[:].rearrange("p (t c i) -> p c t i", t=4, i=4),
                              wd[:].rearrange("p (c i t) -> p c t i", t=4, i=4))
        wd_plane = keep.tile([P, N], U8, name="wd_plane", align_bytes=64)
        nc.vector.tensor_copy(wd_plane[:].rearrange("p (t a c i) -> p a c t i", t=4, a=2, i=16),
                              planes[:, :, WD_SCALES:].rearrange("p a (c i t) -> p a c t i", t=4, i=16))

        sums = keep.tile([P, 4, J], F32, name="sums", align_bytes=64)

        def table_operand(a, first, count):
            start = max(at for at in parted if at <= first)
            words, tokens = parted[start]
            b0 = 2 * (a * tokens + first - start)
            return dict(rhs=words[:, b0 : b0 + 2 * count].bitcast(FP4X4), rhs_scale=planes[:, a, first : first + count])

        def gates(c, gate):
            for u in range(2):
                ga = psum.tile([P, 2, QUARTER], F32, name="ga", bufs=3)
                for e in range(2):
                    t = 2 * u + e
                    for a in range(2):
                        c0 = a * R + t * P
                        nc.tensor.matmul_mx(
                            out=ga[:, e, :], lhsT=wg_dealt[:, 2 * c0 : 2 * (c0 + P)].bitcast(FP4X4),
                            lhsT_scale=planes[:, a, WG_SCALES + t * P : WG_SCALES + (t + 1) * P],
                            start=(a == 0), stop=(a == 1), **table_operand(a, c * QUARTER, QUARTER))
                nc.scalar.activation(gate[:, 2 * u : 2 * u + 2, :], ga[:], SIGMOID)

        def gated(c, s, gate, h):
            ub = psum.tile([P, 4, P], F32, name="ub", bufs=2)
            for t in range(4):
                for a in range(2):
                    c0 = a * R + t * P
                    nc.tensor.matmul_mx(
                        out=ub[:, t, :], lhsT=wu_dealt[:, c0 : c0 + P].bitcast(FP8X4),
                        lhsT_scale=planes[:, a, WU_SCALES + t * P : WU_SCALES + (t + 1) * P],
                        start=(a == 0), stop=(a == 1), **table_operand(a, c * QUARTER + s * P, P))
            nc.vector.tensor_tensor(h[:, 4 * s * P : 4 * (s + 1) * P].rearrange("p (c i t) -> p c t i", i=2, t=4),
                                    ub[:].rearrange("p t (c i) -> p c t i", i=2),
                                    gate[:, :, s * P : (s + 1) * P].rearrange("p t (c i) -> p c t i", i=2), MULT)

        def quantise(h):
            h_codes = ring.tile([P, QUARTER], I32, name="h_codes", align_bytes=64)
            h_scales = ring.tile([P, QUARTER], U8, name="h_scales", align_bytes=64)
            for at in range(0, QUARTER, P):
                nc.vector.quantize_mx(out=h_codes[:, at : at + P].bitcast(FP8X4), scales=h_scales[:, at : at + P],
                                      in_=h[:, 4 * at : 4 * (at + P)])
            return h_codes, h_scales

        ys = keep.tile([P, 4, J], F32, name="ys", align_bytes=64)
        in_bank = {}

        def second_stage(c, h_codes, h_scales):
            banks = [psum.tile([P, 2, QUARTER], F32, name="ga" if c == LAST else "y", bufs=3) for u in range(2)]
            piece = P if c == LAST else QUARTER
            for at in range(0, QUARTER, piece):
                for t in range(4):
                    nc.tensor.matmul_mx(out=banks[t // 2][:, t % 2, at : at + piece],
                                        lhsT=wd_dealt[:, t * P : (t + 1) * P].bitcast(FP8X4),
                                        lhsT_scale=wd_plane[:, t * P : (t + 1) * P],
                                        rhs=h_codes[:, at : at + piece].bitcast(FP8X4),
                                        rhs_scale=h_scales[:, at : at + piece], start=True, stop=True)
            tokens = slice(c * QUARTER, (c + 1) * QUARTER)
            if tokens.start < HALF:
                nc.scalar.copy(ys[:, 0:2, tokens], banks[0][:])
            else:
                in_bank[tokens.start] = banks[0][:, 0, :]
                nc.scalar.copy(ys[:, 1, tokens], banks[0][:, 1, :])
            nc.scalar.copy(ys[:, 2:4, tokens], banks[1][:])

        out_slices = out_0.rearrange("(p t) j -> p t j", t=4)
        rounded = keep.tile([P, J, 4], BF16, name="rounded", align_bytes=64)

        def round_pair(copy, u, first, count):
            copy(rounded[:, first : first + count, 2 * u : 2 * u + 2],
                 sums[:, 2 * u : 2 * u + 2, first : first + count].rearrange("p e j -> p j e"))

        def add_residual(t, first, count):
            nc.vector.tensor_tensor(sums[:, t, first : first + count], windows[t][:].indirect(listed(first, count)),
                                    ys[:, t, first : first + count], ADD)

        for c in range(4):
            h = ring.tile([P, 4 * QUARTER], BF16, name="h", align_bytes=64)
            gate = ring.tile([P, 4, QUARTER], F32, name="gate", align_bytes=64)
            gates(c, gate)
            for s in range(2):
                gated(c, s, gate, h)
            if c > 0:
                second_stage(c - 1, *quantised)
            quantised = quantise(h)
        second_stage(LAST, *quantised)

        early = keep.tile([P, HALF], F32, name="early", align_bytes=64)
        nc.vector.tensor_copy(early[:], windows[0][:].indirect(listed(HALF, HALF)))
        for first in range(0, J, QUARTER):
            if first < HALF:
                add_residual(0, first, QUARTER)
            else:
                nc.vector.tensor_tensor(sums[:, 0, first : first + QUARTER], early[:, first - HALF : first - HALF + QUARTER],
                                        in_bank[first], ADD)
            if first == LAST * QUARTER:
                round_pair(nc.scalar.copy, 0, 0, first)
            add_residual(1, first, QUARTER)
        round_pair(nc.scalar.copy, 0, LAST * QUARTER, QUARTER)
        nc.sync.dma_start(out_slices[:, 0:2, :], sums[:, 0:2, :])
        for first in range(0, J, HALF):
            add_residual(2, first, HALF)
        nc.sync.dma_start(out_slices[:, 2, :], sums[:, 2, :])
        stored = 0
        for first, count in ((0, P), (P, P), (QUARTER, QUARTER), (HALF, P), (HALF + P, P), (LAST * QUARTER, QUARTER)):
            add_residual(3, first, count)
            piece = P if first >= HALF else count
            for at in range(first, first + count, piece):
                round_pair(nc.vector.tensor_copy if at == HALF + P else nc.scalar.copy, 1, at, piece)
            if first + count in (HALF + P, J):
                nc.sync.dma_start(out_slices[:, 3, stored : first + count], sums[:, 3, stored : first + count])
                stored = first + count

        out_codes = keep.tile([P, J], I32, name="out_codes", align_bytes=64)
        out_scales = keep.tile([P, J], U8, name="out_scales", align_bytes=64)
        code_rows = out_1[0].rearrange("p j b -> p (j b)").bitcast(I32)
        stored = 0
        for first, count in ((0, QUARTER), (QUARTER, QUARTER), (HALF, QUARTER), (LAST * QUARTER, P), (J - P, P)):
            part = slice(first, first + count)
            nc.vector.quantize_mx(out=out_codes[:, part].bitcast(FP8X4), scales=out_scales[:, part],
                                  in_=rounded[:, part, :].rearrange("p j t -> p (j t)"))
            if first != HALF:
                nc.sync.dma_start(code_rows[:, stored : part.stop], out_codes[:, stored : part.stop])
                stored = part.stop
        for s in range(4):
            queue = nc.sync if s % 2 == 0 else nc.scalar
            queue.dma_start(out_2[0, s:16:4, :].bitcast(I32), out_scales[s:P:32].bitcast(I32))
